import numpy as np, ml_dtypes
CORES = [3,11,19,27,35,43,51,59]
N = 8
BF = ml_dtypes.bfloat16
W, I, C, V, ST = 4096, 256, 512, 4, 3
def legs(v):
    return np.ascontiguousarray(np.swapaxes(v.reshape(N, 8, 16, I), 2, 3)).astype(np.int32)
def unlegs(v):
    return np.ascontiguousarray(np.swapaxes(v, 2, 3)).reshape(N, 128, I)
def spot(n, al):
    return (((n * (2 * al + 1)) >> 3) + n + 37 * al) & (W - 1)
def pick(x, ix):
    return np.take_along_axis(x, ix.reshape(N, 8, 1, I * 16), 3).reshape(N, 8, 16, I, 16)
def look(x, s, e, l, t, a, b, am):
    run = np.add.accumulate(t, axis=3); tot = run[..., 15:]
    al = (a[..., None] + run) & 255
    be = (b[..., None] + am[:, None, None, None] - (tot - run)) & 255
    f = pick(x, spot(l, al)); g = pick(x, spot(l, be))
    p = s[..., None] + np.add.accumulate(f, axis=4) - f
    q = e[..., None] - (np.add.reduce(g, axis=4, keepdims=True) - np.add.accumulate(g, axis=4) + g)
    d = np.add.reduce(np.minimum(np.abs(p - q), 255), axis=2)
    return f, g, p, tot, d
def parts(rng):
    x = rng.integers(0, 16, (N, 8, 16, W), dtype=np.int32); l = rng.integers(0, W, (N, 8, I, 16), dtype=np.int32); t = rng.integers(0, 256, (N, 8, I, 16), dtype=np.int32)
    a = rng.integers(0, 256, (N, 8, I), dtype=np.int32); c = rng.integers(0, W, (N, 8, 16, C), dtype=np.int32)
    w = rng.integers(0, 256, (N, 8, 16, 1), dtype=np.int32); th = rng.integers(60, 421, (N, 8, I), dtype=np.int32)
    s = rng.integers(0, 136, (N, 8, 16, I), dtype=np.int32)
    closed = rng.random((N, 8, I)) < 0.4
    b = np.where(closed, (a + np.add.reduce(t, axis=3)) & 255, rng.integers(0, 256, (N, 8, I))).astype(np.int32)
    f = look(x, s, s, l, t, a, b, np.zeros(N, np.int32))[0]
    noise = np.rint(rng.standard_normal((N, 8, 16, I)) * rng.choice(np.array([0, 4, 12, 30]), (N, 8, 1, I)))
    e = np.clip(s + np.where(closed[:, :, None, :], np.add.reduce(f, axis=4), 120) + noise, 0, 255).astype(np.int32)
    hit = (rng.random((N, 8, I, 1)) < 0.6) & (np.arange(16) == rng.integers(0, 16, (N, 8, I, 1)))
    t = np.where(hit, (t + rng.integers(1, 256, (N, 8, I, 1))) & 255, t).astype(np.int32)
    return x, s, e, l, t, a, b, c, w, th
def pack(x, s, e, l, t, a, b, c, w, th):
    return {"xt": np.asarray(x, np.float32).reshape(N, 128, W).astype(BF), "sp": np.asarray(s, np.float32).reshape(N, 128, I).astype(BF), "ep": np.asarray(e, np.float32).reshape(N, 128, I).astype(BF),
            "lg": unlegs(np.asarray(l, np.int32)), "tn": unlegs(np.asarray(t, np.int32)), "aa": np.asarray(a, np.int32), "bb": np.asarray(b, np.int32),
            "ct": np.ascontiguousarray(np.asarray(c, np.int32).reshape(N, 128, C)), "wt": np.ascontiguousarray(np.asarray(w, np.int32).reshape(N, 128, 1)), "th": np.asarray(th, np.int32)}
def setup_inputs(rng):
    return pack(*parts(rng))
def setup_inputs_spread(rng):
    x = np.minimum(16 * rng.random((N, 8, 1, W)) ** 0.5 * rng.random((N, 8, 16, W)) ** 0.7, 15).astype(np.int32)
    s = np.minimum(256 * rng.random((N, 8, 1, I)) * rng.random((N, 8, 16, I)) ** 0.5, 255).astype(np.int32)
    e = np.minimum(256 * rng.random((N, 8, 1, I)) ** 0.3 * rng.random((N, 8, 16, I)) ** 0.5, 255).astype(np.int32)
    l = np.minimum(W * rng.random((N, 8, I, 16)) ** rng.choice(np.array([0.25, 1.0, 3.0]), (N, 8, 1, 1)), W - 1).astype(np.int32)
    t = np.minimum(256 * rng.random((N, 8, I, 1)) * rng.random((N, 8, I, 16)), 255).astype(np.int32)
    a = np.minimum(256 * rng.random((N, 8, I)) ** 2, 255).astype(np.int32); b = rng.integers(0, 256, (N, 8, I))
    c = np.minimum(W * rng.random((N, 8, 16, C)) ** rng.choice(np.array([0.25, 1.0, 3.0]), (N, 8, 1, C)), W - 1).astype(np.int32)
    w = np.exp2(8 * rng.random((N, 8, 16, 1))).astype(np.int32) - 1; th = np.minimum(np.exp2(4 + 8 * rng.random((N, 8, I))).astype(np.int32) - 1, 4080)
    return pack(x, s, e, l, t, a, b, c, w, th)
def setup_inputs_ends(rng):
    share = rng.choice(np.array([0.03, 0.3, 0.5, 0.7, 0.97]), (N, 8, 1, 1)); share[0, 0] = 0.0; share[N - 1, 7] = 1.0
    x = 15 * (np.where(rng.random((N, 8, 1, W)) < 0.3, rng.random((N, 8, 16, W)), rng.random((N, 8, 1, W))) < share)
    alike = rng.random((N, 8, 1, I)) < 0.5
    s = 255 * np.where(alike, rng.integers(0, 2, (N, 8, 1, I)), rng.integers(0, 2, (N, 8, 16, I)))
    e = 255 * np.where(alike, rng.integers(0, 2, (N, 8, 1, I)), rng.integers(0, 2, (N, 8, 16, I)))
    for i, lo, hi in ((0, 255, 0), (1, 0, 255), (2, 0, 0), (I - 3, 0, 0), (I - 2, 0, 255), (I - 1, 255, 0)): s[..., i] = lo; e[..., i] = hi
    l = (W - 1) * rng.integers(0, 2, (N, 8, I, 16)); t = 255 * rng.integers(0, 2, (N, 8, I, 16)); l[:, :, I - 1] = W - 1; t[:, :, I - 1] = 255; l[:, :, 0] = 0; t[:, :, 0] = 0
    a = 255 * rng.integers(0, 2, (N, 8, I)); b = 255 * rng.integers(0, 2, (N, 8, I)); c = (W - 1) * rng.integers(0, 2, (N, 8, 16, C))
    w = 255 * rng.integers(0, 2, (N, 8, 16, 1)); w[:, 7] = 255; w[:, 3] = 0
    th = 4080 * rng.integers(0, 2, (N, 8, I)); th[:, ::2, I - 1] = 4080; th[:, 1::2, I - 1] = 0; th[:, 7, I - 1] = 4080 * (np.arange(N) & 1); th[:, 7, 0] = 4080 - th[:, 7, I - 1]
    return pack(x, s, e, l, t, a, b, c, w, th)
def setup_inputs_corners(rng):
    x, s, e, l, t, a, b, c, w, th = parts(rng)
    x[:, 1] = 7; e[:, 1, :, ::2] = np.minimum(s[:, 1, :, ::2] + 112, 255)
    x[:, 3] = 15 * (rng.random((N, 1, W)) < 0.5)
    l[:, 2] = rng.choice(np.array([0, W - 1, W // 2]), (N, I, 16)); c[:, 2] = rng.choice(np.array([0, W - 1, 1]), (N, 16, C)); l[:, 4] = rng.choice(np.array([0, W - 1, 5]), (N, I, 1))
    w[:, 5] = 0; w[:, 6] = 255; w[:, 0] = 255 * rng.integers(0, 2, (N, 16, 1))
    t[:, :, ::8, 0] = (t[:, :, ::8, 0] + 1) & 255; t[:, :, 4::8, 15] = (t[:, :, 4::8, 15] + 255) & 255
    m = np.min(look(x, s, e, l, t, a, b, np.zeros(N, np.int32))[4], axis=3)
    th = np.clip(m + rng.integers(-1, 2, m.shape), 0, 4080)
    return pack(x, s, e, l, t, a, b, c, w, th)
def setup_inputs_crowd(rng):
    x, s, e, l, t, a, b, c, w, th = parts(rng)
    w[:, 0] = 0; w[:, 1] = 255; s[:, 1] = 255
    w[:, 2] = 0; w[:, 2, 0] = 1; s[:, 2, 0] = 254 + rng.integers(0, 2, (N, I))
    w[:, 3] = 0; w[:, 3, 0] = 255; s[:, 3, 0] = 255
    for q in range(N): s[q, 3, 0, rng.integers(0, I)] = 1
    s[:, :, 0] = np.maximum(s[:, :, 0], 1); e[:, :, 0] = np.minimum(e[:, :, 0], s[:, :, 0] - 1)
    for q in range(N):
        g = int(rng.integers(0, 8)); i = int(rng.integers(0, I))
        if q < 4:
            th[q] = (0, 0, 4080, 4080)[q]
            if q & 1: th[q, g, i] = 4080 - th[q, g, i]
        else:
            th[q] = 4080 * rng.integers(0, 2, (8, 1)); th[q, g, i] = 4080 - th[q, g, i]; th[q, (g + 3) % 8, I - 1] = 4080 - th[q, (g + 3) % 8, I - 1]
    return pack(x, s, e, l, t, a, b, c, w, th)
def setup_inputs_falls(rng):
    x, s, e, l, t, a, b, c, w, th = parts(rng)
    e = np.minimum(np.maximum(e, s), s + 200)
    th[:] = 4079; x[:, 5, 0] = 0
    x[:, 6] = 15 - ((rng.integers(0, 16, (N, 1, W)) == np.arange(16)[:, None]) & (rng.random((N, 1, W)) < 0.03125)).astype(np.int32)
    z = rng.random((N, 1, I)) < 0.5; s[:, 6] = np.where(z, 0, s[:, 6]); e[:, 6] = np.where(z, 0, e[:, 6])
    q = int(rng.integers(0, N))
    for i in range(N):
        o = (q - ST * i) % N; n = 32 * int(rng.integers(0, I // 8)) + int(rng.integers(1, 32))
        n = (n, 0, n, 8 * I)[i & 3]
        m = (rng.permutation(8 * I) < n).reshape(8, 1, I)
        s[o] = np.where(m, 255, s[o]); e[o] = np.where(m, 0, e[o])
        near = ~m[5, 0] & (rng.random(I) < 0.25)
        s[o, 5] = np.where(near, 255, s[o, 5]); e[o, 5] = np.where(near, 0, e[o, 5]); s[o, 5, 0] = np.where(near, 254, s[o, 5, 0])
    return pack(x, s, e, l, t, a, b, c, w, th)
def check_inputs(d):
    bad = []
    for k, hi in (("xt", 15), ("sp", 255), ("ep", 255), ("lg", W - 1), ("tn", 255), ("aa", 255), ("bb", 255), ("ct", W - 1), ("wt", 255), ("th", 4080)):
        v = np.asarray(d[k]).astype(np.float64)
        if not (np.min(v) >= 0 and np.max(v) <= hi): bad.append("range of " + k)
        elif np.any(v != np.floor(v)): bad.append("whole numbers in " + k)
    return bad
def reference(xt, sp, ep, lg, tn, aa, bb, ct, wt, th):
    x = xt.astype(np.float32).astype(np.int32).reshape(N, 8, 16, W)
    s = sp.astype(np.float32).astype(np.int32).reshape(N, 8, 16, I); e = ep.astype(np.float32).astype(np.int32).reshape(N, 8, 16, I)
    l = legs(lg); t = legs(tn); a = aa.astype(np.int32); b = bb.astype(np.int32)
    c = ct.astype(np.int32).reshape(N, 8, 16, C); w = wt.astype(np.int32).reshape(N, 8, 16, 1)
    am = np.zeros(N, np.int32); leg = np.arange(16); slot = np.arange(I)
    for v in range(V):
        h = (np.arange(N) - ST * v) % N
        l0, t0, a0, b0 = l[h], t[h], a[h], b[h]
        f, g, p, tot, d = look(x, s[h], e[h], l0, t0, a0, b0, am)
        k = np.argmin(d, axis=3); ok = np.min(d, axis=3) <= th
        at = k[:, :, None, :, None]
        pk, fk, gk = [np.take_along_axis(z, at, 4)[..., 0] for z in (p, f, g)]
        u = np.add.reduce(w * np.minimum(pk, 255), axis=2)
        got = np.swapaxes(np.take_along_axis(c, (u % C)[:, :, None, :], 3), 2, 3)
        t[h] = np.where(ok[..., None] & (leg == k[..., None]), (t0 + (b0 + am[:, None, None] - a0)[..., None] - tot) & 255, t0)
        l[h] = np.where(~ok[..., None] & (leg <= k[..., None]), got, l0)
        pc = np.broadcast_to(((C // I) * slot + u % (C // I))[:, :, None, :], (N, 8, 16, I))
        np.put_along_axis(c, pc, np.where(ok[:, :, None, :], np.take_along_axis(c, pc, 3), np.swapaxes(l0, 2, 3)), 3)
        px = np.broadcast_to(((W // I) * slot + u % (W // I))[:, :, None, :], (N, 8, 16, I))
        np.put_along_axis(x, px, (fk + gk) >> 1, 3)
        am = (np.add.reduce((~ok).astype(np.int32), axis=(1, 2)) & 31).astype(np.int32)
    return {"yx": x.reshape(N, 128, W).astype(np.float32).astype(BF), "yl": unlegs(l).astype(np.float32), "yt": unlegs(t).astype(np.float32), "yc": c.reshape(N, 128, C).astype(np.float32)}

@@ -1,0 +1,852 @@
+import numpy as np
+from concourse.bass import DstId, RemoteDMATransfer
+from concourse.mybir import AluOpType, ActivationFunctionType
+
+NV, STEP, ROT = 4, 3, 167
+CHOICE = {"groups": [[64, 64], [64, 64]], "gv": {("B", 0), ("F", 1, 0)}, "zs": set(), "ab": {2, 3}, "ev": set(),
+          "cut": {(k, c) for k in "FB" for c in range(4)}, "sp": {0, 1}, "hv": set(), "k1": {0}, "dzs": False,
+          "wv": {0, 1}}
+COSTS = [{"g": 1.55, "sc": 3.5, "pe": 0.0005, "lat": 0.1, "rl": 2.5, "bw": 60e3},
+         {"g": 1.1, "sc": 5.0, "pe": 0.0005, "lat": 0.15, "rl": 3.5, "bw": 40e3},
+         {"g": 2.0, "sc": 2.5, "pe": 0.0005, "lat": 0.06, "rl": 2.0, "bw": 80e3},
+         {"g": 1.55, "sc": 3.5, "pe": 0.0008, "lat": 0.1, "rl": 3.0, "bw": 50e3}]
+ROUNDS, POLISH, SEED = 1500, 5000, 0
+FW = 4096 + 16 * 4
+
+SCRATCH = {
+    "x": ("sbuf", [128, 4272], "bfloat16"),
+    "F": ("sbuf", [128, FW], "bfloat16"), "B": ("sbuf", [128, FW], "bfloat16"),
+    "PX": ("sbuf", [128, FW], "bfloat16"), "Y": ("sbuf", [128, FW], "bfloat16"),
+    "Zp": ("sbuf", [128, 16, 16, 16], "bfloat16"), "Zn": ("sbuf", [128, 16, 16, 16], "bfloat16"),
+    "pmask": ("sbuf", [128, 2048], "bfloat16"),
+    "cn": ("sbuf", [128, 1024], "float32"), "db": ("sbuf", [128, 512], "float32"),
+    "lf0": ("sbuf", [128, 256], "uint16"), "lf1": ("sbuf", [128, 256], "uint16"), "lb": ("sbuf", [128, 256], "uint16"),
+    "l1": ("sbuf", [128, 16], "uint16"), "l2": ("sbuf", [128, 16], "uint16"), "l3": ("sbuf", [128, 16], "uint16"),
+    "l4": ("sbuf", [128, 16], "uint16"), "l5": ("sbuf", [128, 16], "uint16"),
+    "rf": ("sbuf", [128, 256], "int32"), "rb": ("sbuf", [128, 256], "int32"), "hh": ("sbuf", [128, 256], "int32"),
+    "svF": ("sbuf", [128, 256], "bfloat16"), "svB": ("sbuf", [128, 256], "bfloat16"),
+    "ms": ("sbuf", [128, 256], "float32"), "mp": ("sbuf", [128, 256], "bfloat16"),
+    "fk": ("sbuf", [128, 256], "bfloat16"), "fb": ("sbuf", [128, 256], "bfloat16"), "av": ("sbuf", [128, 256], "bfloat16"),
+    "ki": ("sbuf", [128, 16], "int32"), "of": ("sbuf", [128, 16], "int32"), "k2": ("sbuf", [128, 16], "int32"),
+    "cd": ("sbuf", [128, 16], "int32"), "nok": ("sbuf", [128, 16], "bfloat16"), "us": ("sbuf", [128, 16], "float32"),
+    "ui": ("sbuf", [128, 16], "int32"), "u9": ("sbuf", [128, 16], "int32"), "u4": ("sbuf", [128, 16], "int32"),
+    "y4": ("sbuf", [128, 16], "int32"), "u1": ("sbuf", [128, 16], "int32"), "c1": ("sbuf", [128, 16], "float32"),
+    "c2": ("sbuf", [128, 16], "float32"), "c3": ("sbuf", [128, 16], "float32"),
+    "cq": ("sbuf", [128, 128], "bfloat16"), "m32": ("sbuf", [128, 2], "bfloat16"), "idm": ("sbuf", [128, 128], "float32"),
+    "o256": ("sbuf", [128, 128], "bfloat16"),
+    "arow": ("sbuf", [128, 128], "bfloat16"),
+    "hb": ("sbuf", [128, 256], "bfloat16"), "c192": ("sbuf", [128, 128], "bfloat16"), "m192": ("sbuf", [128, 128], "bfloat16"),
+    "tni": ("sbuf", [128, 256], "int32"), "lgi": ("sbuf", [128, 256], "int32"), "abi": ("sbuf", [128, 512], "int32"),
+    "spb": ("sbuf", [128, 256], "bfloat16"), "epb": ("sbuf", [128, 256], "bfloat16"), "wti": ("sbuf", [128, 1], "int32"),
+    "thi": ("sbuf", [128, 256], "int32"), "cti": ("sbuf", [128, 512], "int32"),
+    "tnb": ("sbuf", [128, 256], "bfloat16"), "abb": ("sbuf", [128, 512], "bfloat16"), "thf": ("sbuf", [128, 256], "float32"),
+    "thk": ("sbuf", [128, 16], "float32"), "col": ("sbuf", [128, 16], "float32"), "coli": ("sbuf", [128, 4], "int32"),
+    "wb": ("sbuf", [128, 2], "bfloat16"),
+    "ioc": ("sbuf", [128, 144], "float32"), "iog": ("sbuf", [128, 128], "float32"), "ioj": ("sbuf", [128, 128], "float32"),
+    "iot": ("sbuf", [128, 256], "float32"),
+    "idb": ("sbuf", [128, 128], "bfloat16"), "idn": ("sbuf", [128, 128], "bfloat16"), "idf": ("sbuf", [128, 128], "float32"),
+    "Dm": ("sbuf", [128, 128], "float32"), "Dd": ("sbuf", [128, 128], "float32"), "tm1": ("sbuf", [128, 128], "float32"),
+    "tm2": ("sbuf", [128, 128], "float32"), "tm3": ("sbuf", [128, 128], "float32"),
+    "blk": ("sbuf", [128, 128], "bfloat16"), "tri": ("sbuf", [128, 128], "bfloat16"),
+    "sel8": ("sbuf", [128, 128], "bfloat16"), "sel0": ("sbuf", [128, 128], "bfloat16"), "e8": ("sbuf", [128, 144], "float32"),
+    "c45": ("sbuf", [128, 128], "bfloat16"), "c9": ("sbuf", [128, 128], "bfloat16"),
+    "Zpos": ("sbuf", [128, 144], "bfloat16"), "Zneg": ("sbuf", [128, 144], "bfloat16"), "ZW": ("sbuf", [128, 144], "bfloat16"),
+    "kh": ("sbuf", [128, 128], "bfloat16"), "kl": ("sbuf", [128, 128], "bfloat16"), "rst": ("sbuf", [128, 128], "float32"),
+    "M3": ("sbuf", [128, 32], "float32"), "M1": ("sbuf", [128, 32], "float32"), "M2": ("sbuf", [128, 32], "float32"),
+    "rbase": ("sbuf", [128, 16], "float32"), "cbase": ("sbuf", [128, 16], "float32"),
+    "onb": ("sbuf", [128, 256], "bfloat16"), "onf": ("sbuf", [128, 128], "float32"),
+    "oL": ("sbuf", [128, 256], "float32"), "oT": ("sbuf", [128, 256], "float32"), "ng": ("sbuf", [128, 256], "float32"),
+    "oC": ("sbuf", [128, 512], "float32"),
+}
+for _v in range(NV + 1):
+    SCRATCH["st%d" % _v] = ("sbuf", [128, 512], "float32")
+for _v in range(NV):
+    SCRATCH["sb%d" % _v] = ("sbuf", [128, 1024], "bfloat16")
+    SCRATCH["eb%d" % _v] = ("sbuf", [128, 512], "float32")
+for _n in ("pc0", "pc1", "pk0", "pk1", "pu", "pw", "pb", "pm"):
+    SCRATCH[_n] = ("psum", [128, 512], "float32")
+SEMAPHORES = ["cV", "cS", "cP", "cG", "sent"] + ["d%d" % i for i in range(40)] + ["r%d" % i for i in range(24)]
+
+CY = 0.00083 * 1.2
+A_ = AluOpType
+ACT = ActivationFunctionType
+
+
+def build(g, T, topo, core, rank, par):
+    ops = []
+    cnt = {"d": 0, "r": 0}
+    prev = {}
+    ctx = {"v": -1, "g": 0, "c": 0}
+    V, S, P = g.vector, g.scalar, g.tensor
+
+    def add(eng, dur, rd, wr, fn, bank=(), lat=0.0, kind="c", name="", after=None):
+        ops.append({"at": (ctx["v"], ctx["g"], ctx["c"]), "eng": eng, "dur": dur, "rd": list(rd), "wr": list(wr), "fn": fn, "bank": list(bank), "lat": lat,
+                    "kind": kind, "name": name, "after": after, "sem": None})
+        return len(ops) - 1
+
+    def vc(n, c=1.0):
+        return max(64.0, n * c) * CY + 0.02
+
+    def ts(out, in0, s1, op0, rd, wr, n, s2=None, op1=None, c=1.0, bank=(), name="ts"):
+        if op1 is None:
+            fn = lambda: V.tensor_scalar(out, in0, s1, None, op0)
+        else:
+            fn = lambda: V.tensor_scalar(out, in0, s1, s2, op0, op1)
+        return add("V", vc(n, c), rd, wr, fn, bank, name=name)
+
+    def tt(out, in0, in1, op, rd, wr, n, c=2.0, bank=(), name="tt"):
+        return add("V", vc(n, c), rd, wr, lambda: V.tensor_tensor(out, in0, in1, op), bank, name=name)
+
+    def cp(out, in_, rd, wr, n, c=1.0, bank=(), name="cp"):
+        return add("V", vc(n, c), rd, wr, lambda: V.tensor_copy(out, in_), bank, name=name)
+
+    def ms_(out, val, wr, n, c=1.0):
+        return add("V", vc(n, c), [], wr, lambda: V.memset(out, val), name="memset")
+
+    def act(out, in_, func, rd, wr, n, bias=0.0, scale=1.0, c=1.0, bank=(), name="act"):
+        return add("S", vc(n, c) + 0.03, rd, wr, lambda: S.activation(out, in_, func, bias=bias, scale=scale), bank, name=name)
+
+    def mm(lst, rd, wr, bank, name="mm"):
+        def fn():
+            last = None
+            for o, l, r, s0, s1, _c in lst:
+                last = P.matmul(o, l, r, s0, s1)
+            return last
+        return add("P", sum(m[5] for m in lst) * par["pe"] + 0.03, rd, wr, fn, [bank], name=name)
+
+    def iota(out, pat, base, cm, wr, n, flt=True):
+        if flt:
+            fn = lambda: g.iota(out, pat, base, cm, allow_small_or_imprecise_dtypes=True)
+        else:
+            fn = lambda: g.iota(out, pat, base, cm)
+        return add("G", 0.156 + 2 * n * CY, [], wr, fn, name="iota")
+
+    def gcp(out, in_, rd, wr, n, name="gcp"):
+        return add("G", 0.2 + 2 * n * CY, rd, wr, lambda: g.affine_select(out, in_, [[0, n]], A_.is_ge, 0.0, 0, 0), name=name)
+
+    def dma(q, out, in_, rd, wr, nbytes, name="dma"):
+        qq = g.sync if q == "Y" else S
+        i = add(q, 0.06, rd, wr, lambda: qq.dma_start(out, in_), lat=1.8 + nbytes / 180e3, kind="d", name=name,
+                after=None if rd else prev.get(q))
+        prev[q] = i
+        ops[i]["sem"] = ("d%d" % cnt["d"], 16)
+        cnt["d"] += 1
+        return i
+
+    def send(dst_rank, srcs, dst, rd, key, nbytes, name, after=None):
+        dc = T.cores[dst_rank]
+        rid, pid, _e = topo.addr(dc)
+        m = topo.mask(core, dc)
+        ne = len(topo.engines(core, dc))
+        sem = "r%d" % cnt["r"]
+        cnt["r"] += 1
+        if len(srcs) == 1:
+            fn = lambda: g.remote_dma(dst, srcs[0], T.sem[sem], T.sem.sent, pid, rid, m)
+        else:
+            fn = lambda: g.remote_dma_fused([RemoteDMATransfer(dst_ids=[DstId(rid=rid, pnc=pid)], dma_engine_mask=m,
+                                                               remote_sem=T.sem[sem], srcs=srcs, dsts=[dst], alu_op=1)],
+                                            local_sem=T.sem.sent)
+        i = add("G", 0.8, rd, [], fn, kind="s", name=name, after=after)
+        ops[i]["ne"] = ne
+        j = add(None, 0.0, [], [key], None, lat=par["rl"] + nbytes / par["bw"], kind="r", name="arr" + name, after=i)
+        ops[j]["sem"] = (sem, ne)
+        return i
+
+    grp, chunks, t = [], [], 0
+    for gi, sizes in enumerate(par["groups"]):
+        g0 = t
+        cs = []
+        for n in sizes:
+            cs.append(len(chunks))
+            chunks.append({"g": gi, "t0": t, "t1": t + n, "n": n, "pos": 16 * (gi + 1) + 16 * t, "first": t == g0})
+            t += n
+        grp.append({"t0": g0, "t1": t, "n": t - g0, "pos": 16 * (gi + 1) + 16 * g0, "cs": cs, "q0": g0 // 16, "q1": t // 16})
+    NG = len(grp)
+    col = T.col
+    PC, JC, GC, G15, P1, N15, N256, P16, P1615, J32, J16, J2, WC, CW = [col[:, i:i + 1] for i in range(14)]
+
+    dma("Y", T.tni[:], T.tn[:], [], ["tni"], 131072)
+    dma("S", T.abi[0:8, 0:256], T.aa[:], [], ["ai"], 8192)
+    dma("S", T.abi[0:8, 256:512], T.bb[:], [], ["bi"], 8192)
+    dma("Y", T.lgi[:], T.lg[:], [], ["lgi"], 131072)
+    dma("Y", T.x[:, ROT:4096], T.xt[:, 0:4096 - ROT], [], ["x"], 1350000)
+    dma("S", T.x[:, 0:ROT], T.xt[:, 4096 - ROT:4096], [], ["x2"], 50000)
+    dma("S", T.spb[:], T.sp[:], [], ["spb"], 500000)
+    dma("S", T.epb[:], T.ep[:], [], ["epb"], 600000)
+    dma("S", T.wti[:], T.wt[:], [], ["wti"], 50000)
+    dma("S", T.thi[0:8, :], T.th[:], [], ["thi"], 50000)
+    dma("Y", T.cti[:], T.ct[:], [], ["cti"], 1650000)
+
+    iota(T.coli[:, 0:1], [[0, 1]], 0, 1, ["coli0"], 1, False)
+    iota(T.iog[:], [[1, 8], [0, 16]], 0, 0, ["iog"], 128)
+    iota(T.ioc[:], [[1, 144]], 0, 0, ["ioc"], 144)
+    iota(T.ioj[:], [[0, 8], [1, 16]], 0, 0, ["ioj"], 128)
+    cp(PC, T.coli[:, 0:1], ["coli0"], ["PC"], 1)
+    ts(T.coli[:, 1:2], T.coli[:, 0:1], 4, A_.arith_shift_right, ["coli0"], ["coli1"], 1)
+    ts(T.coli[:, 2:3], T.coli[:, 0:1], 15, A_.bitwise_and, ["coli0"], ["coli2"], 1)
+    cp(GC, T.coli[:, 1:2], ["coli1"], ["GC"], 1)
+    cp(JC, T.coli[:, 2:3], ["coli2"], ["JC"], 1)
+    ts(G15, T.coli[:, 1:2], 16.0, A_.mult, ["coli1"], ["G15"], 1, 15.0, A_.add)
+    ts(P1, T.coli[:, 0:1], 1.0, A_.add, ["coli0"], ["P1"], 1)
+    ts(N15, T.coli[:, 2:3], 15.0, A_.is_equal, ["coli2"], ["N15"], 1, -1.0, A_.mult)
+    ts(N256, T.coli[:, 2:3], 15.0, A_.not_equal, ["coli2"], ["N256"], 1, -256.0, A_.mult)
+    ts(P16, T.coli[:, 0:1], 16.0, A_.mult, ["coli0"], ["P16"], 1)
+    ts(P1615, T.coli[:, 0:1], 16.0, A_.mult, ["coli0"], ["P1615"], 1, 15.0, A_.add)
+    ts(J32, T.coli[:, 2:3], 32.0, A_.mult, ["coli2"], ["J32"], 1)
+    ts(J16, T.coli[:, 2:3], 16.0, A_.mult, ["coli2"], ["J16"], 1)
+    ts(J2, T.coli[:, 2:3], 4.0, A_.mult, ["coli2"], ["J2"], 1)
+    ioc = T.ioc[:, 0:128]
+    ts(T.blk[:], T.iog[:], GC, A_.is_equal, ["iog", "GC"], ["blk"], 128)
+    ts(T.tm3[:], T.iog[:], GC, A_.is_equal, ["iog", "GC"], ["tm3"], 128, 1.0 / 256, A_.mult)
+    add("G", 0.2 + 256 * CY, ["tm3"], ["tri"],
+        lambda: g.affine_select(T.tri[:], T.tm3[:], [[1, 128]], A_.is_ge, 0.0, 0, -1), name="tri")
+    ts(T.sel8[0:8, :], T.iog[0:8, :], col[0:8, 0:1], A_.is_equal, ["iog", "PC"], ["sel8"], 128, 1.0 / 256, A_.mult)
+    ms_(T.c9[0:1, :], 9.0 / 512, ["c9"], 128, 0.5)
+    ms_(T.onb[:], 1.0, ["onb"], 256, 0.5)
+    ms_(T.arow[0:1, :], 0.0, ["arow"], 128, 0.5)
+    ms_(T.m192[:], -192.0, ["m192"], 128, 0.5)
+    ms_(T.m32[0:1, :], 20.0, ["m32"], 2, 0.5)
+    ms_(T.o256[:], 1.0 / 256, ["o256"], 128, 0.5)
+    iota(T.iot[0:2, 0:128], [[0, 128]], 12288, -12255, ["iot0"], 128)
+    ts(T.c192[0:2, :], T.iot[0:2, 0:128], 1.0 / 64, A_.mult, ["iot0"], ["c192"], 128)
+    ts(T.idb[:], ioc, PC, A_.is_equal, ["ioc", "PC"], ["idb"], 128)
+    ts(T.idn[:], ioc, PC, A_.is_equal, ["ioc", "PC"], ["idn"], 128, -1.0, A_.mult)
+    ts(T.idf[:], ioc, PC, A_.is_equal, ["ioc", "PC"], ["idf"], 128)
+    if par["dzs"]:
+        ts(T.idm[:], ioc, PC, A_.is_equal, ["ioc", "PC"], ["idm"], 128, -1.0, A_.mult)
+    ts(T.tm1[:], T.iog[:], GC, A_.is_equal, ["iog", "GC", "N15"], ["tm1"], 128, N15, A_.mult)
+    tt(T.Dm[:], T.tm1[:], T.idf[:], A_.add, ["tm1", "idf"], ["Dm"], 128)
+    ts(T.tm2[:], ioc, P1, A_.is_equal, ["ioc", "P1", "N256"], ["tm2"], 128, N256, A_.mult)
+    ts(T.tm1[:], ioc, PC, A_.is_equal, ["ioc", "PC"], ["tm1"], 128, 256.0, A_.mult)
+    tt(T.Dd[:], T.tm1[:], T.tm2[:], A_.add, ["tm1", "tm2"], ["Dd"], 128)
+    ts(T.sel0[0:8, :], T.ioc[0:8, 0:128], col[0:8, 7:8], A_.is_equal, ["ioc", "P16"], ["sel0"], 128, -1.0, A_.mult)
+    ts(T.e8[0:8, :], T.ioc[0:8, :], col[0:8, 8:9], A_.is_equal, ["ioc", "P1615"], ["e8"], 144)
+    ts(T.c45[0:1, :], T.ioj[0:1, :], 0.0, A_.is_equal, ["ioj"], ["c45"], 128, -4.5, A_.mult)
+    ts(T.Zpos[:], T.ioc[:], G15, A_.is_equal, ["ioc", "G15"], ["Zpos"], 144, 4096.0, A_.mult)
+    ts(T.Zneg[:], T.ioc[:], G15, A_.is_equal, ["ioc", "G15"], ["Zneg"], 144, -4096.0, A_.mult)
+    ts(WC, T.wti[:], 2.0, A_.mult, ["wti"], ["WC"], 1)
+    cp(T.wb[:, 0:1], WC, ["WC"], ["wb"], 1)
+    ts(T.ZW[:], T.ioc[:], G15, A_.is_equal, ["ioc", "G15", "WC"], ["ZW"], 144, WC, A_.mult)
+    mm([(T.pu[:, 64:65], T.blk[:], T.wb[:, 0:1], True, True, 64)], ["blk", "wb"], ["pu_cw"], "pu")
+    ts(CW, T.pu[:, 64:65], 255.0, A_.mult, ["pu_cw"], ["CW"], 1, bank=["pu"])
+    iota(T.iot[:, 0:128], [[512, 8], [0, 16]], 0, 0, ["iot0"], 128)
+    ts(T.kh[:], T.iot[:, 0:128], J32, A_.add, ["iot0", "J32"], ["kh"], 128)
+    ts(T.kl[:], T.ioj[:], 2.0, A_.mult, ["ioj"], ["kl"], 128)
+    ts(T.rst[:], T.ioj[:], 0.0, A_.is_equal, ["ioj"], ["rst"], 128, 33554432.0, A_.mult)
+    iota(T.iot[:, 128:160], [[1, 16], [100, 2]], 0, 0, ["iot1"], 32)
+    ts(T.M1[:], T.iot[:, 128:160], JC, A_.is_le, ["iot1", "JC"], ["M1"], 32)
+    ts(T.M2[:], T.iot[:, 128:160], -100.0, A_.add, ["iot1", "JC"], ["M2"], 32, JC, A_.is_ge)
+    ts(T.M3[:], T.M2[:], 1.0 / 64, A_.mult, ["M2"], ["M3"], 32)
+    ts(T.rbase[:], T.ioc[:, 0:16], 256.0, A_.mult, ["ioc", "J16"], ["rbase"], 16, J16, A_.add)
+    ts(T.rbase[:], T.rbase[:], float(ROT), A_.add, ["rbase"], ["rbase"], 16)
+    ts(T.cbase[:], T.ioc[:, 0:16], 64.0, A_.mult, ["ioc", "J2"], ["cbase"], 16, J2, A_.add)
+    nmax = 16 * max(c["n"] for c in chunks)
+    ms_(T.pmask[:, 0:nmax], 1.0, ["pmask"], nmax, 0.5)
+    ms_(T.pmask[:, 15:nmax:16], 0.0, ["pmask"], nmax // 16, 0.5)
+    for ci, c in enumerate(chunks):
+        ms_(T.PX[:, c["pos"]:c["pos"] + 1], 0.0, ["PX0%d" % ci], 1)
+    for gi, G in enumerate(grp):
+        ms_(T.F[:, G["pos"] - 1:G["pos"]], 0.0, ["Fpad%d" % gi], 1)
+        ms_(T.B[:, G["pos"] - 1:G["pos"]], 0.0, ["Bpad%d" % gi], 1)
+
+    def stn(v, G):
+        return T["st%d" % v][:, 2 * G["t0"]:2 * G["t0"] + G["n"]]
+
+    def stw(v, G):
+        return T["st%d" % v][:, 2 * G["t0"] + G["n"]:2 * G["t1"]]
+
+    cp(T.tnb[:], T.tni[:], ["tni"], ["tnb"], 256)
+    cp(T.abb[0:8, 0:256], T.abi[0:8, 0:256], ["ai"], ["ab"], 256)
+    cp(T.abb[0:8, 256:512], T.abi[0:8, 256:512], ["bi"], ["bb"], 256)
+    mm([(T.pb[:, 0:256], T.c9[0:1, :], T.onb[0:1, :], True, False, 256),
+        (T.pb[:, 0:256], T.sel8[0:8, :], T.abb[0:8, 0:256], False, False, 256),
+        (T.pb[:, 0:256], T.tri[:], T.tnb[:], False, True, 256)], ["c9", "onb", "sel8", "ab", "tri", "tnb"],
+       ["pb%d" % i for i in range(NG)], "pb")
+    for gi, G in enumerate(grp):
+        sl = slice(G["t0"], G["t1"])
+        ts(T.hh[:, sl], T.pb[:, sl], -0.515625, A_.add, ["pb%d" % gi], ["hh%d" % gi], G["n"], bank=["pb"])
+        tt(stw(0, G), T.pb[:, sl], T.hh[:, sl], A_.subtract, ["pb%d" % gi, "hh%d" % gi], ["st0w%d" % gi], G["n"], 1.0, ["pb"])
+        ts(stn(0, G), T.lgi[:, sl], 64.0, A_.mult, ["lgi"], ["st0n%d" % gi], G["n"], 9472.0625, A_.add)
+    sb0 = T.sb0
+    mm([(T.pk1[:, 0:256], T.sel8[0:8, :], T.abb[0:8, 256:512], True, True, 256)], ["sel8", "bb"], ["pk1"], "pk1")
+    act(sb0[:, 768:1024], T.pk1[:, 0:256], ACT.Identity, ["pk1"], ["sb0b"], 256, bias=-255.0 / 512, bank=["pk1"])
+    ts(sb0[:, 0:256], T.spb[:], -1.0, A_.mult, ["spb"], ["sb0s"], 256, 255.0, A_.add, 0.5)
+    lst = [(T.pk0[:, 0:256], T.idb[:], T.spb[:], True, False, 256), (T.pk0[:, 0:256], T.idn[:], T.epb[:], False, False, 256)]
+    for c in chunks:
+        o = T.pk0[:, c["t0"] + 1:c["t1"]]
+        lst.append((o, T.idn[:], T.spb[:, c["t0"]:c["t1"] - 1], False, False, c["n"]))
+        lst.append((o, T.idb[:], T.epb[:, c["t0"]:c["t1"] - 1], False, c is chunks[-1], c["n"]))
+    mm(lst, ["idb", "idn", "spb", "epb"], ["pk0"], "pk0")
+    act(sb0[:, 256:512], T.pk0[:, 0:256], ACT.Identity, ["pk0"], ["sb0h"], 256, bank=["pk0"])
+    tt(sb0[:, 512:768], T.pk0[:, 0:256], sb0[:, 256:512], A_.subtract, ["pk0", "sb0h"], ["sb0l"], 256, 1.0, ["pk0"])
+    cp(T.thf[0:8, :], T.thi[0:8, :], ["thi"], ["thf"], 256)
+    mm([(T.pm[:, 0:16], T.e8[0:8, 15 - r:143 - r], T.thf[0:8, r:256:16], r == 0, r == 15, 256) for r in range(16)],
+       ["e8", "thf"], ["pm"], "pm")
+    ts(T.thk[:], T.pm[:, 0:16], 4096.0, A_.mult, ["pm"], ["thk"], 16, 4095.0, A_.add, bank=["pm"])
+    iota(T.cn[:, 0:1024:2], [[0, 512]], 0, 0, ["cn"], 512)
+    ts(T.cn[:, 1:1024:2], T.cti[:], 64.0, A_.mult, ["cti"], ["cn"], 512, 9472.0625, A_.add)
+
+    gc_, sc_ = par["g"], par["sc"]
+    last_send = None
+    nr = len(T.cores)
+    for v in range(NV):
+        last = v == NV - 1
+        ctx.update({"v": v, "g": 0, "c": 0})
+        sb = T["sb%d" % v]
+        kS, kH, kL, kB = (["sb0s"], ["sb0h"], ["sb0l"], ["sb0b"]) if v == 0 else (["sb%d" % v],) * 4
+        lf = T["lf%d" % (v & 1)]
+        eb = T["eb%d" % v]
+        XK = ["x", "x2"]
+        if not last:
+            last_send = send((rank + STEP) % nr, [sb[:]], T["sb%d" % (v + 1)][:], kS + kH + kL + kB, "sb%d" % (v + 1), 262144,
+                             "stat%d" % v, last_send)
+        else:
+            gcp(T.x[:, 4096:4096 + ROT], T.x[:, 0:ROT], XK + ["xg"], ["xw"], ROT)
+            XK = XK + ["xg"]
+        for gi, G in enumerate(grp):
+            n, sl = G["n"], slice(G["t0"], G["t1"])
+            kn, kw = (["st0n%d" % gi], ["st0w%d" % gi]) if v == 0 else (["st%d_%d" % (v, gi)],) * 2
+            if v and gi in par["sp"]:
+                kn = ["sn%d_%d" % (v, gi)]
+            ctx["g"] = gi
+            G["kn"], G["kw"] = kn, kw
+            bk = ("pb", "pw")[gi & 1]
+            pa, pz, kz = T[bk][:, 256 + G["t0"]:256 + G["t1"]], T[bk][:, sl], ["pb%d" % gi]
+            mm([(pa, T.idf[:], stw(v, G), True, True, 4 * n)], ["idf"] + kw, ["pw%d" % gi], bk, "wcopy")
+            tt(T.rf[:, sl], stn(v, G), pa, A_.mult, kn + ["pw%d" % gi], ["rf%d" % gi], n, 1.0, [bk], "prodF")
+            ts(T.rf[:, sl], T.rf[:, sl], 4095, A_.bitwise_and, ["rf%d" % gi], ["rf%d" % gi], n, name="andF")
+            cp(lf[:, sl], T.rf[:, sl], ["rf%d" % gi], ["lf%d_%d" % (v & 1, gi)], n, name="u16F")
+            bs, ka = sb[:, 768 + G["t0"]:768 + G["t1"]], ["pw%d" % gi]
+            if gi in par["wv"]:
+                mm([(pz, T.Dm[:], stw(v, G), True, False, 4 * n), (pz, T.idb[:], bs, False, False, n),
+                    (pz, T.c192[0:2, :], T.onb[0:2, 0:n], False, False, n)], ["Dm", "idb", "c192", "onb"] + kw + kB, kz, bk, "w0b")
+                mm([(pz, T.arow[0:1, :], T.onb[0:1, 0:n], False, True, n)], ["arow", "onb"], kz, bk, "w0bA")
+                if gi in par["hv"]:
+                    ts(T.hb[:, sl], pz, -0.515625, A_.add, kz, ["hb%d" % gi], n, bank=[bk], name="h")
+                else:
+                    act(T.hb[:, sl], pz, ACT.Identity, kz, ["hb%d" % gi], n, bias=-0.515625, bank=[bk], name="h")
+                tt(pz, pz, T.hb[:, sl], A_.subtract, kz + ["hb%d" % gi], kz, n, 1.0, [bk], "wb")
+            else:
+                mm([(pa, T.Dm[:], stw(v, G), True, False, 4 * n), (pa, T.idb[:], bs, False, False, n)], ["Dm", "idb"] + kw + kB, ka, bk, "w0b")
+                mm([(pa, T.arow[0:1, :], T.onb[0:1, 0:n], False, True, n)], ["arow", "onb"], ka, bk, "w0bA")
+                if gi in par["hv"]:
+                    ts(T.hb[:, sl], pa, 192.0, A_.add, ka, ["hb%d" % gi], n, bank=[bk], name="h")
+                else:
+                    act(T.hb[:, sl], pa, ACT.Identity, ka, ["hb%d" % gi], n, bias=192.0, bank=[bk], name="h")
+                mm([(pz, T.Dm[:], stw(v, G), True, False, 4 * n), (pz, T.idb[:], bs, False, False, n),
+                    (pz, T.arow[0:1, :], T.onb[0:1, 0:n], False, False, n), (pz, T.c192[0:2, :], T.onb[0:2, 0:n], False, False, n),
+                    (pz, T.idn[:], T.hb[:, sl], False, True, n)],
+                   ["Dm", "idb", "arow", "c192", "onb", "idn", "hb%d" % gi] + kw + kB, kz, bk, "wb")
+            tt(T.rb[:, sl], stn(v, G), pz, A_.mult, kn + kz, ["rb%d" % gi], n, 1.0, [bk], "prodB")
+            ts(T.rb[:, sl], T.rb[:, sl], 4095, A_.bitwise_and, ["rb%d" % gi], ["rb%d" % gi], n, name="andB")
+            cp(T.lb[:, sl], T.rb[:, sl], ["rb%d" % gi], ["lb%d" % gi], n, name="u16B")
+            dzo = T.db[:, 2 * G["t0"] + n:2 * G["t1"]]
+            if par["dzs"]:
+                mm([(pz, T.idm[:], stw(v, G), False, True, 4 * n)], ["idm"] + kw, kz, bk, "dzm")
+                act(dzo, pz, ACT.Identity, kz, ["dz%d" % gi], n, bank=[bk], name="dz")
+            else:
+                tt(dzo, pz, stw(v, G), A_.subtract, kz + kw, ["dz%d" % gi], n, 1.0, [bk], "dz")
+        mm([(T.pu[:, 0:16], T.ZW[:, 15 - r:143 - r], sb[:, r:256:16], r == 0, r == 15, 64) for r in range(16)],
+           ["ZW"] + kS, ["pu_s"], "pu", "usmm")
+        act(T.us[:], T.pu[:, 0:16], ACT.Identity, ["pu_s", "CW"], ["us"], 16, bias=CW, scale=-1.0, bank=["pu"], name="us")
+        for gi, G in enumerate(grp):
+            pk, kk = T["pk%d" % (gi & 1)], "pk%d" % (gi & 1)
+            for ci in G["cs"]:
+                c = chunks[ci]
+                ctx.update({"g": gi, "c": ci})
+                n, p, t0, t1 = c["n"], c["pos"], c["t0"], c["t1"]
+                e = p + 16 * n
+                Fk, Bk = ["F%d" % ci, "Fl%d" % ci, "Fa%d" % ci], ["B%d" % ci, "Bl%d" % ci, "Ba%d" % ci]
+                Fp = "Fpad%d" % gi if c["first"] else "Fl%d" % (ci - 1)
+                Bp = "Bpad%d" % gi if c["first"] else "Bl%d" % (ci - 1)
+                for kind, buf, lst_, lk, wk in (("F", T.F, lf, "lf%d_%d" % (v & 1, gi), Fk), ("B", T.B, T.lb, "lb%d" % gi, Bk)):
+                    pieces = [(0, n, wk)]
+                    if (kind, ci) in par["cut"]:
+                        pieces = [(0, n // 2, wk[2:]), (n // 2, n, wk[:2])]
+                    for h, (i0, i1, wk2) in enumerate(pieces):
+                        win = T.x[:, 0:4096].indirect(lst_[:, t0 + i0:t0 + i1])
+                        o, nm = buf[:, p + 16 * i0:p + 16 * i1], "g%s%d%s" % (kind, ci, "ab"[h])
+                        if (kind, ci) in par["gv"] or (kind, ci, h) in par["gv"]:
+                            cp(o, win, XK + [lk], wk2, 16 * (i1 - i0), gc_, name=nm)
+                        else:
+                            act(o, win, ACT.Identity, XK + [lk], wk2, 16 * (i1 - i0), c=gc_, name=nm)
+                slF, slB = T.F[:, p - 1:e - 16:16], T.B[:, p - 1:e - 16:16]
+                Fb, Bb = [Fp, Fk[0], Fk[2]], [Bp, Bk[0], Bk[2]]
+                gcp(T.svF[:, t0:t1], slF, Fb, ["svF%d" % ci], n, "saveF")
+                add("V", vc(16 * n, 0.5), Fb[1:] + ["pmask"], ["PX%d" % ci],
+                    lambda p=p, e=e, n=n: V.tensor_tensor_scan(T.PX[:, p + 1:e], T.F[:, p:e - 1], T.pmask[:, 0:16 * n - 1], 0.0,
+                                                               A_.add, A_.mult), name="scanP%d" % ci)
+                gcp(slF, sb[:, 256 + t0:256 + t1], kH, Fb, n, "hi")
+                pc, kc = T["pc%d" % (ci & 1)], "pc%d" % (ci & 1)
+                mm([(pc[:, 0:n], T.idb[:], sb[:, 512 + t0:512 + t1], True, False, n),
+                    (pc[:, 1:n], T.idn[:], T.PX[:, p + 15:e - 16:16], False, False, n)],
+                   ["idb", "idn", "PX%d" % ci] + kL, [kc], kc, "corr0")
+                lst = [(pc[:, 0:n], T.idb[:], T.B[:, p + j:e:16], False, False, max(n, 64)) for j in range(16)]
+                lst.append((pc[:, 1:n], T.idn[:], T.B[:, p + 15:e - 16:16], False, True, max(n, 64)))
+                mm(lst, ["idb", "idn"] + Bk, [kc], kc, "corr%d" % ci)
+                gcp(T.svB[:, t0:t1], slB, Bb, ["svB%d" % ci], n, "saveB")
+                if ci in par["ev"]:
+                    ts(slB, pc[:, 0:n], -1.0, A_.mult, [kc], Bb, n, bank=[kc], name="evac")
+                else:
+                    act(slB, pc[:, 0:n], ACT.Identity, [kc], Bb, n, scale=-1.0, bank=[kc], name="evac")
+                add("V", vc(16 * n, 0.5), Fb + Bb, ["Y%d" % ci],
+                    lambda p=p, e=e: V.tensor_tensor_scan(T.Y[:, p:e], T.F[:, p - 1:e - 1], T.B[:, p - 1:e - 1], 0.0,
+                                                          A_.add, A_.subtract), name="scanY%d" % ci)
+                q0, q1 = t0 // 16, t1 // 16
+                ko = pk[:, t0 - G["t0"]:t1 - G["t0"]]
+                lo_, hi_ = t0 - G["t0"], t1 - G["t0"]
+                if ci in par["ab"]:
+                    ts(T.Y[:, p:e], T.Y[:, p:e], 255.0, A_.min, ["Y%d" % ci], ["Y%d" % ci], 16 * n, c=0.5, name="zm%d" % ci)
+                    act(T.Zp[:, q0:q1], T.Y[:, p:e], ACT.Abs, ["Y%d" % ci], ["Zp%d" % ci], 16 * n, name="za%d" % ci)
+                    mm([(ko, T.idb[:], T.kh[:, lo_:hi_], True, False, n), (ko, T.idb[:], T.kl[:, lo_:hi_], False, False, n)],
+                       ["idb", "kh", "kl"], [kk], kk, "key0")
+                    mm([(ko, T.Zpos[:, 15 - r:143 - r], T.Zp[:, q0:q1, r, :], False, r == 15, max(n, 64)) for r in range(16)],
+                       ["Zpos", "Zp%d" % ci], [kk], kk, "keyp")
+                    continue
+                ts(T.Zp[:, q0:q1], T.Y[:, p:e], 0.0, A_.max, ["Y%d" % ci], ["Zp%d" % ci], 16 * n, 255.0, A_.min, 0.5, name="zp%d" % ci)
+                if ci in par["zs"]:
+                    act(T.Zn[:, q0:q1], T.Y[:, p:e], ACT.Relu, ["Y%d" % ci], ["Zn%d" % ci], 16 * n, scale=-1.0, name="zn%d" % ci)
+                    Zw = T.Zpos
+                else:
+                    ts(T.Zn[:, q0:q1], T.Y[:, p:e], 0.0, A_.min, ["Y%d" % ci], ["Zn%d" % ci], 16 * n, c=0.5, name="zn%d" % ci)
+                    Zw = T.Zneg
+                lst = [(ko, T.idb[:], T.kh[:, lo_:hi_], True, False, n), (ko, T.idb[:], T.kl[:, lo_:hi_], False, False, n)]
+                mm(lst, ["idb", "kh", "kl"], [kk], kk, "key0")
+                mm([(ko, T.Zpos[:, 15 - r:143 - r], T.Zp[:, q0:q1, r, :], False, False, max(n, 64)) for r in range(16)],
+                   ["Zpos", "Zp%d" % ci], [kk], kk, "keyp")
+                mm([(ko, Zw[:, 15 - r:143 - r], T.Zn[:, q0:q1, r, :], False, r == 15, max(n, 64)) for r in range(16)],
+                   ["Zpos", "Zneg", "Zn%d" % ci], [kk], kk, "keyn")
+            n, p, t0, t1 = G["n"], G["pos"], G["t0"], G["t1"]
+            e = p + 16 * n
+            sl, qs, Q, s = slice(t0, t1), slice(G["q0"], G["q1"]), G["q1"] - G["q0"], str(gi)
+            Fall = [k % ci for ci in G["cs"] for k in ("Fa%d", "F%d", "Fl%d")]
+            Ball = [k % ci for ci in G["cs"] for k in ("Ba%d", "B%d", "Bl%d")]
+            gcp(T.F[:, p + 15:e - 16:16], T.svF[:, t0 + 1:t1], ["svF%d" % ci for ci in G["cs"]], Fall[:-1], n - 1, "restF")
+            gcp(T.B[:, p + 15:e - 16:16], T.svB[:, t0 + 1:t1], ["svB%d" % ci for ci in G["cs"]], Ball[:-1], n - 1, "restB")
+            add("V", vc(n), [kk, "rst"], ["ms" + s],
+                lambda sl=sl, n=n, pk=pk: V.tensor_tensor_scan(T.ms[:, sl], T.rst[:, 0:n], pk[:, 0:n], 0.0, A_.add, A_.min),
+                [kk], name="minscan")
+            mk = T.ms[:, t0 + 15:t1:16]
+            tt(T.nok[:, qs], mk, T.thk[:, qs], A_.is_gt, ["ms" + s, "thk"], ["nok" + s], Q, name="nok")
+            if gi in par["k1"]:
+                tt(T.ki[:, qs], mk, T.nok[:, qs], A_.add, ["ms" + s, "nok" + s], ["ki" + s], Q, name="ki")
+            else:
+                cp(T.ki[:, qs], mk, ["ms" + s], ["ki" + s], Q, name="ki")
+            ts(T.of[:, qs], T.ki[:, qs], 4095, A_.bitwise_and, ["ki" + s], ["of" + s], Q, 1, A_.logical_shift_right, name="of")
+            cp(T.l1[:, qs], T.of[:, qs], ["of" + s], ["l1" + s], Q, name="l1")
+            if gi in par["k1"]:
+                ts(T.cd[:, qs], T.ki[:, qs], 31, A_.bitwise_and, ["ki" + s], ["cd" + s], Q, name="cd")
+            else:
+                ts(T.k2[:, qs], T.ki[:, qs], 31, A_.bitwise_and, ["ki" + s], ["k2" + s], Q, name="k2")
+                tt(T.cd[:, qs], T.k2[:, qs], T.nok[:, qs], A_.add, ["k2" + s, "nok" + s], ["cd" + s], Q, name="cd")
+            cp(T.l2[:, qs], T.cd[:, qs], ["cd" + s], ["l2" + s], Q, name="l2")
+            if not last:
+                mm([(T.pm[0:1, 0:128], T.m32[0:1, 0:1], T.onb[0:1, 0:128], True, False, 128)][:1 if gi == 0 else 0]
+                   + [(T.pm[0:1, 0:128], T.nok[:, q:q + 1], T.o256[:], False, q == 15, 128) for q in range(G["q0"], G["q1"])],
+                   ["nok" + s, "onb", "o256", "m32"], ["pm"], "pm", "count")
+            PXall = [k % ci for ci in G["cs"] for k in ("PX%d", "PX0%d")]
+            tt(T.mp[:, sl], T.PX[:, p:e].indirect(T.l1[:, qs]), sb[:, sl], A_.min, PXall + ["l1" + s] + kS, ["mp" + s], n, gc_, name="mp")
+            uo = T.pu[:, 16 + G["q0"]:16 + G["q1"]]
+            mm([(uo, T.idb[:], T.nok[:, qs], True, False, 64)], ["idb", "nok" + s], ["pu" + s], "pu", "umm0")
+            mm([(uo, T.ZW[:, 15 - r:143 - r], T.mp[:, t0 + r:t1:16], False, r == 15, 64) for r in range(16)],
+               ["ZW", "mp" + s], ["pu" + s], "pu", "umm")
+            tt(T.ui[:, qs], uo, T.us[:, qs], A_.add, ["pu" + s, "us"], ["ui" + s], Q, bank=["pu"], name="ui")
+            ts(T.u9[:, qs], T.ui[:, qs], 1022, A_.bitwise_and, ["ui" + s], ["u9" + s], Q, name="u9")
+            ts(T.l3[:, qs], T.u9[:, qs], 1.0, A_.add, ["u9" + s], ["l3" + s], Q, name="l3")
+            ts(T.u4[:, qs], T.ui[:, qs], 1, A_.logical_shift_right, ["ui" + s], ["u4" + s], Q, 15, A_.bitwise_and, name="u4")
+            tt(T.y4[:, qs], T.u4[:, qs], T.rbase[:, qs], A_.add, ["u4" + s, "rbase"], ["y4" + s], Q, name="y4")
+            w0 = 0
+            if last:
+                w0 = (16 * t0 + ROT) // 16 * 16
+            elif 16 * t1 + ROT > 4096:
+                ts(T.y4[:, qs], T.y4[:, qs], 4095, A_.bitwise_and, ["y4" + s], ["y4" + s], Q, name="y4and")
+            G["w0"] = w0
+            ts(T.l4[:, qs], T.y4[:, qs], float(-w0), A_.add, ["y4" + s], ["l4" + s], Q, name="l4")
+            act(T.fk[:, sl], T.F[:, p:e].indirect(T.l1[:, qs]), ACT.Identity, Fall + ["l1" + s], ["fk" + s], n, c=gc_, name="fk")
+            act(T.fb[:, sl], T.B[:, p:e].indirect(T.l1[:, qs]), ACT.Identity, Ball + ["l1" + s], ["fb" + s], n, c=gc_, name="fb")
+            mm([(pk[:, 0:n], T.idb[:], T.fk[:, sl], True, False, n), (pk[:, 0:n], T.idb[:], T.fb[:, sl], False, True, n)],
+               ["idb", "fk" + s, "fb" + s], [kk], kk, "fbsum")
+            act(T.av[:, sl], pk[:, 0:n], ACT.Identity, [kk], ["av" + s], n, bias=191.75, scale=0.5, bank=[kk], name="av")
+            a0, a1, a2 = 2 * t0, 2 * t0 + n, 2 * t1
+            tt(eb[:, a1:a2], T.M1[:].indirect(T.l2[:, qs]), T.db[:, a1:a2], A_.mult, ["M1", "l2" + s, "dz" + s], ["ez%d_%d" % (v, gi)], n,
+               gc_, name="ez")
+            tt(T.db[:, a0:a1], T.cn[:].indirect(T.l3[:, qs]), stn(v, G), A_.subtract, ["cn", "l3" + s] + G["kn"], ["dl" + s], n,
+               gc_, name="dl")
+            M2 = T.M3 if last else T.M2
+            tt(eb[:, a0:a1], M2[:].indirect(T.l2[:, qs]), T.db[:, a0:a1], A_.mult, ["M2", "M3", "l2" + s, "dl" + s],
+               ["el%d_%d" % (v, gi)], n, gc_, name="el")
+            dst = (rank - STEP * v) % nr if last else (rank + STEP) % nr
+            if last:
+                act(T.oL[:, sl], stn(v, G), ACT.Identity, G["kn"], ["oL" + s], n, bias=-148.0009765625, scale=1.0 / 64, name="oL")
+                last_send = send(dst, [stw(v, G), eb[:, a1:a2]], stw(NV, G), G["kw"] + ["ez%d_%d" % (v, gi)], "st%d_%d" % (NV, gi),
+                                 512 * n, "homew%d" % gi, last_send)
+                last_send = send(dst, [T.oL[:, sl], eb[:, a0:a1]], stn(NV, G), ["oL" + s, "el%d_%d" % (v, gi)], "home%d" % gi,
+                                 512 * n, "homen%d" % gi, last_send)
+                continue
+            if gi in par["sp"]:
+                last_send = send(dst, [stw(v, G), eb[:, a1:a2]], stw(v + 1, G), G["kw"] + ["ez%d_%d" % (v, gi)],
+                                 "st%d_%d" % (v + 1, gi), 512 * n, "dynw", last_send)
+                last_send = send(dst, [stn(v, G), eb[:, a0:a1]], stn(v + 1, G), G["kn"] + ["el%d_%d" % (v, gi)],
+                                 "sn%d_%d" % (v + 1, gi), 512 * n, "dynn", last_send)
+                continue
+            last_send = send(dst, [T["st%d" % v][:, a0:a2], eb[:, a0:a2]], T["st%d" % (v + 1)][:, a0:a2],
+                             G["kn"] + G["kw"] + ["ez%d_%d" % (v, gi), "el%d_%d" % (v, gi)], "st%d_%d" % (v + 1, gi), 1024 * n,
+                             "dyn%d_%d" % (v, gi), last_send)
+        if not last:
+            act(T.cq[0:1, :], T.pm[0:1, 0:128], ACT.Identity, ["pm"], ["cq"], 128, bias=-15.5 / 256, bank=["pm"], name="cq")
+            tt(T.arow[0:1, :], T.pm[0:1, 0:128], T.cq[0:1, :], A_.subtract, ["pm", "cq"], ["arow"], 128, 1.0, ["pm"], "arow")
+        for gi, G in enumerate(grp):
+            s, sl, qs = str(gi), slice(G["t0"], G["t1"]), slice(G["q0"], G["q1"])
+            if last:
+                w1 = G["w0"] + 16 * G["n"] + 16
+                wk = ["xs%d" % gi] + (["xs%d" % (gi + 1)] if gi + 1 < NG else ["xw"])
+                tt(T.x[:, G["w0"]:w1].indirect(T.l4[:, qs]), T.av[:, sl], T.m192[:, 0:G["n"]], A_.add, ["l4" + s, "av" + s, "m192"],
+                   wk + ["xg"], G["n"], sc_, name="scx")
+                c0 = ROT if gi == 0 else G["w0"]
+                c1 = grp[gi + 1]["w0"] if gi + 1 < NG else 4096 + ROT
+                dma("Y", T.yx[:, c0 - ROT:c1 - ROT], T.x[:, c0:c1], ["xs%d" % gi] + ([] if gi + 1 < NG else ["xw"]), [], 256 * (c1 - c0), "yx")
+            else:
+                tt(T.x[:, 0:4096].indirect(T.l4[:, qs]), T.av[:, sl], T.m192[:, 0:G["n"]], A_.add, ["l4" + s, "av" + s, "m192"], XK,
+                   G["n"], sc_, name="scx")
+        allg = lambda k: [k + str(i) for i in range(NG)]
+        ts(T.u1[:], T.ui[:], 3, A_.bitwise_and, allg("ui"), ["u1"], 16, name="u1")
+        tt(T.c3[:], T.u1[:], T.cbase[:], A_.add, ["u1", "cbase"], ["c3"], 16, name="c3")
+        cp(T.l5[:], T.c3[:], ["c3"], ["l5"], 16, name="l5")
+        for gi, G in enumerate(grp):
+            cp(T.cn[:].indirect(T.l5[:, G["q0"]:G["q1"]]), stn(v, G), ["l5"] + G["kn"], ["cn"], G["n"], sc_, name="scc")
+
+    act(T.oC[:], T.cn[:, 1:1024:2], ACT.Identity, ["cn"], ["oC"], 512, bias=-148.0009765625, scale=1.0 / 64, name="oC")
+    dma("Y", T.yc[:], T.oC[:], ["oC"], [], 262144, "yc")
+    for gi, G in enumerate(grp):
+        n, sl, s, k = G["n"], slice(G["t0"], G["t1"]), str(gi), ["st%d_%d" % (NV, gi)]
+        bk = ("pw", "pb")[gi & 1]
+        pt = T[bk][:, 0:n]
+        mm([(pt, T.c45[0:1, :], T.onb[0:1, 0:n], True, False, n), (pt, T.sel0[0:8, :], T.abb[0:8, sl], False, False, n)],
+           ["c45", "onb", "sel0", "ab"], [z + str(i) for i in range(NG) for z in ("pb", "pw")][:0] + [bk + "0"], bk, "fin0")
+        mm([(pt, T.Dd[:], stw(NV, G), False, True, 4 * n)], ["Dd"] + k, [bk + "0"], bk, "fin1")
+        ts(T.ng[:, sl], pt, 0.0, A_.is_lt, [bk + "0"], ["ng" + s], n, 256.0, A_.mult, bank=[bk], name="ng")
+        tt(T.oT[:, sl], pt, T.ng[:, sl], A_.add, [bk + "0", "ng" + s], ["oT" + s], n, 1.0, [bk], "oT")
+        dma("Y", T.yt[:, sl], T.oT[:, sl], ["oT" + s], [], 512 * n, "yt")
+        dma("S", T.yl[:, sl], stn(NV, G), ["home" + s], [], 512 * n, "yl")
+    return ops
+
+
+def depend(ops):
+    lastw, readers, bank = {}, {}, {}
+    for i, o in enumerate(ops):
+        d = {}
+
+        def need(j, hard):
+            if j is not None and j != i:
+                if ops[j]["eng"] == "P" and o["eng"] == "P":
+                    hard = False
+                d[j] = d.get(j, False) or hard
+        for k in o["rd"]:
+            need(lastw.get(k), True)
+        for k in o["wr"]:
+            need(lastw.get(k), True)
+            for j in readers.get(k, []):
+                need(j, True)
+        for b in o["bank"]:
+            j = bank.get(b)
+            if j is not None:
+                need(j[0], ops[j[0]]["eng"] != o["eng"])
+                if j[1] is not None:
+                    need(j[1], ops[j[1]]["eng"] != o["eng"])
+            other = None if j is None else (j[0] if ops[j[0]]["eng"] != o["eng"] else j[1])
+            bank[b] = (i, other)
+        need(o["after"], False)
+        for k in o["rd"]:
+            readers.setdefault(k, []).append(i)
+        for k in o["wr"]:
+            lastw[k] = i
+            readers[k] = []
+        o["dep"] = d
+
+
+def gaps(ops, lat):
+    out = []
+    for o in ops:
+        out.append([(j, ops[j]["dur"] + ((ops[j]["lat"] + lat) if hard else 0.0)) for j, hard in o["dep"].items()])
+    return out
+
+
+def place(n, eng, dur, pred, succ, key, first=None):
+    left = [len(p) for p in pred]
+    ready = [i for i in range(n) if left[i] == 0]
+    beg = [0.0] * n
+    busy = {}
+    while ready:
+        a = min(ready, key=lambda i: key[i])
+        ready.remove(a)
+        s = first[a] if first else 0.0
+        for j, d in pred[a]:
+            if beg[j] + d > s:
+                s = beg[j] + d
+        if eng[a] is not None:
+            iv = busy.setdefault(eng[a], [])
+            k = len(iv)
+            while k > 0 and iv[k - 1][1] > s:
+                k -= 1
+            while k < len(iv) and iv[k][0] < s + dur[a]:
+                s = max(s, iv[k][1])
+                k += 1
+            iv.insert(k, (s, s + dur[a]))
+        beg[a] = s
+        for j, _d in succ[a]:
+            left[j] -= 1
+            if left[j] == 0:
+                ready.append(j)
+    return beg
+
+
+LATE = {"scc": 6.0, "us": 3.0, "usmm": 3.0, "dz": 3.0, "dzm": 3.0, "u1": 5.0, "c3": 5.0, "l5": 5.0}
+
+
+def first_keys(ops):
+    key = []
+    first = {}
+    for o in ops:
+        if o["name"][:2] == "gF":
+            first.setdefault(o["at"][1], o["at"][2])
+    for i, o in enumerate(ops):
+        v, gi, ci = o["at"]
+        nm = o["name"]
+        if nm in ("wcopy", "prodF", "andF", "u16F", "w0b", "w0bA", "h", "wb", "prodB", "andB", "u16B", "dz", "dzm"):
+            k = 3.3 * first[gi] - 3.5
+        elif nm[:2] == "gF":
+            k = 3.3 * ci - 1.7
+        elif nm[:2] == "gB":
+            k = 3.3 * ci
+        elif nm[:4] in ("stat", "arrs", "us", "usmm"):
+            k = 0.0
+        elif nm == "saveF" or nm == "hi" or nm == "corr0" or nm[:5] == "scanP":
+            k = 3.3 * ci + 0.1
+        elif nm[:4] in ("corr", "save", "evac") or nm[:5] == "scanY":
+            k = 3.3 * ci + 1.55
+        elif nm[0] == "z" or nm[:3] == "key":
+            k = 3.3 * ci + 3.0
+        else:
+            k = 3.3 * ci + 4.8
+        key.append(20.0 * v + k + LATE.get(nm, 0.0) + 1e-3 * i)
+    return key
+
+
+def span(ops, pred, order):
+    beg, free, end = [0.0] * len(ops), {}, 0.0
+    for i in order:
+        o = ops[i]
+        s = free.get(o["eng"], 0.0)
+        for j, d in pred[i]:
+            if beg[j] + d > s:
+                s = beg[j] + d
+        beg[i] = s
+        if o["eng"] is not None:
+            free[o["eng"]] = s + o["dur"]
+        end = max(end, s + o["dur"] + o["lat"])
+    return end, beg
+
+
+def improve(variants, lat, rounds, seed):
+    ops = variants[0]
+    n = len(ops)
+    eng, dur = [o["eng"] for o in ops], [o["dur"] for o in ops]
+    preds = [gaps(v, l) for v, l in zip(variants, lat)]
+    pred = preds[0]
+    succ = [[] for _ in range(n)]
+    rpred = [[] for _ in range(n)]
+    for i in range(n):
+        for j, d in pred[i]:
+            succ[j].append((i, d))
+            rpred[j].append((i, d - dur[j] + dur[i]))
+    tail = [o["lat"] for o in ops]
+    rng = np.random.default_rng(seed)
+    key = first_keys(ops)
+    best, cur, bkey, border = 1e9, 1e9, key, None
+    tag = np.array([o["name"] for o in ops])
+    names = sorted(set(tag.tolist()))
+    starts = [i for i in range(n) if ops[i]["name"] == "wcopy" and ops[i - 1]["name"] != "dz"]
+    per = starts[2] - starts[1]
+    for it in range(rounds):
+        passes = 0
+        if it:
+            k = np.array(bkey)
+            mode = int(rng.integers(0, 4))
+            if mode == 0:
+                k = k + rng.normal(0.0, float(rng.choice([0.1, 0.3, 1.0])), n) * (rng.random(n) < 0.2)
+            elif mode == 1:
+                for nm in rng.choice(names, int(rng.integers(1, 5))):
+                    k = k + rng.normal(0.0, 1.5) * (tag == nm)
+            else:
+                a = int(rng.integers(0, per))
+                w = int(rng.integers(1, 30))
+                sh = rng.normal(0.0, 2.0)
+                for s in starts:
+                    if mode == 2 or rng.random() < 0.4:
+                        k[s + a:s + a + w] += sh
+            key = [float(x) for x in k]
+            passes = int(rng.integers(0, 2))
+        for _ in range(passes):
+            beg = place(n, eng, dur, pred, succ, key)
+            rb = place(n, eng, dur, rpred, pred, [-(beg[i] + dur[i] + tail[i]) for i in range(n)], tail)
+            key = [-(rb[i] + dur[i]) for i in range(n)]
+        beg = place(n, eng, dur, pred, succ, key)
+        order = sorted(range(n), key=lambda i: (beg[i], i))
+        val = sum(span(v, p, order)[0] for v, p in zip(variants, preds)) / len(variants)
+        if val < cur + 0.6 * (1.0 - it / rounds) * rng.random():
+            cur, bkey = val, beg
+        if val < best:
+            best, border = val, order
+    return border, best
+
+
+def polish(variants, lat, order, rounds, seed):
+    ops = variants[0]
+    n = len(ops)
+    preds = [gaps(v, l) for v, l in zip(variants, lat)]
+    eng = [o["eng"] for o in ops]
+    durs = [[o["dur"] for o in v] for v in variants]
+    tails = [[o["dur"] + o["lat"] for o in v] for v in variants]
+    pset = [set(o["dep"]) for o in ops]
+    rng = np.random.default_rng(seed)
+
+    def run(order, w):
+        pred, dur, tail = preds[w], durs[w], tails[w]
+        beg, why, free, lastop = [0.0] * n, [-1] * n, {}, {}
+        end, ei = 0.0, -1
+        for i in order:
+            e = eng[i]
+            s, y = free.get(e, 0.0), lastop.get(e, -1)
+            for j, d in pred[i]:
+                if beg[j] + d >= s:
+                    s, y = beg[j] + d, j
+            beg[i], why[i] = s, y
+            if e is not None:
+                free[e], lastop[e] = s + dur[i], i
+            if s + tail[i] > end:
+                end, ei = s + tail[i], i
+        return end, why, ei
+
+    def arcs(res):
+        out = []
+        for _e, why, i in res:
+            while why[i] >= 0:
+                if why[i] not in pset[i]:
+                    out.append((why[i], i))
+                i = why[i]
+        return out
+    res = [run(order, w) for w in range(len(variants))]
+    cur = sum(r[0] for r in res)
+    best, border, cand = cur, order, arcs(res)
+    for it in range(rounds):
+        u, v = cand[int(rng.integers(0, len(cand)))]
+        a, b = order.index(u), order.index(v)
+        mid = order[a:b + 1]
+        if rng.random() < 0.5:
+            for _ in range(int(rng.integers(0, 3))):
+                k = a - 1
+                while k >= 0 and eng[order[k]] != eng[v]:
+                    k -= 1
+                if k >= 0:
+                    a = k
+            mid = order[a:b + 1]
+            take = {v}
+            for i in reversed(mid):
+                if i in take:
+                    take |= pset[i]
+            if mid[0] in take:
+                continue
+            new = [i for i in mid if i in take] + [i for i in mid if i not in take]
+        else:
+            for _ in range(int(rng.integers(0, 3))):
+                k = b + 1
+                while k < n and eng[order[k]] != eng[u]:
+                    k += 1
+                if k < n:
+                    b = k
+            mid = order[a:b + 1]
+            take = {u}
+            for i in mid:
+                if pset[i] & take:
+                    take.add(i)
+            if mid[-1] in take:
+                continue
+            new = [i for i in mid if i not in take] + [i for i in mid if i in take]
+        o2 = order[:a] + new + order[b + 1:]
+        res = [run(o2, w) for w in range(len(variants))]
+        val = sum(r[0] for r in res)
+        if val <= cur + 0.5 * (1.0 - it / rounds) * rng.random():
+            order, cur, cand = o2, val, arcs(res)
+            if val < best:
+                best, border = val, o2
+    return border, best / len(variants)
+
+
+def emit(g, T, ops, order):
+    qs = {"V": g.vector, "S": g.scalar, "P": g.tensor, "G": g, "Y": g.sync}
+    count = {"V": 0, "S": 0, "P": 0, "G": 0}
+    known = {e: {} for e in qs}
+    clock = {}
+    total = {}
+    sent = 0
+    for i in order:
+        o = ops[i]
+        if o["kind"] == "r":
+            clock[i] = {o["sem"][0]: o["sem"][1]}
+            total[o["sem"][0]] = o["sem"][1]
+            continue
+        e = o["eng"]
+        kn = known[e]
+        want = [j for j, hard in o["dep"].items() if hard]
+        want.sort(key=lambda j: -ops[j].get("pos", -1))
+        for j in want:
+            sem, val = ops[j]["sem"]
+            if kn.get(sem, 0) < val:
+                qs[e].wait_ge(T.sem[sem], val)
+                for k2, v2 in clock[j].items():
+                    if kn.get(k2, 0) < v2:
+                        kn[k2] = v2
+        ins = o["fn"]()
+        o["pos"] = len(clock)
+        if o["kind"] == "s":
+            sent += o["ne"]
+            clock[i] = dict(kn)
+            continue
+        if o["kind"] == "c":
+            count[e] += 1
+            o["sem"] = ("c" + e, count[e])
+            ins.then_inc(T.sem["c" + e], 1)
+        else:
+            ins.then_inc(T.sem[o["sem"][0]], 16)
+        clock[i] = dict(kn)
+        clock[i][o["sem"][0]] = o["sem"][1]
+        total[o["sem"][0]] = o["sem"][1]
+    g.wait_ge(T.sem.sent, sent)
+    for sem, val in total.items():
+        if max(known[e].get(sem, 0) for e in qs) < val:
+            g.sync.wait_ge(T.sem[sem], val)
+
+
+PLAN = {}
+
+
+def rank_program(g, core, T, topo):
+    rank = T.rank_of(core)
+    if rank is None:
+        return
+    variants = make(g, T, topo, core, rank, CHOICE, 1 if "order" in PLAN else len(COSTS))
+    if "order" not in PLAN:
+        lat = [c["lat"] for c in COSTS]
+        PLAN["order"] = polish(variants, lat, improve(variants, lat, ROUNDS, SEED)[0], POLISH, SEED)[0]
+    emit(g, T, variants[0], PLAN["order"])
+
+
+def make(g, T, topo, core, rank, choice, k):
+    out = []
+    for c in COSTS[:k]:
+        par = dict(c)
+        par.update(choice)
+        ops = build(g, T, topo, core, rank, par)
+        depend(ops)
+        out.append(ops)
+    return out

@@ -3,14 +3,13 @@ from concourse.bass import DstId, RemoteDMATransfer
 from concourse.mybir import AluOpType, ActivationFunctionType
 
 NV, STEP, ROT = 4, 3, 167
-CHOICE = {"groups": [[64, 64], [64, 64]], "gv": {("B", 0), ("F", 1, 0)}, "zs": set(), "ab": {2, 3}, "ev": set(),
+CHOICE = {"groups": [[64, 64], [64, 64]], "gv": {("B", 0)}, "zs": {3}, "ab": {2}, "ev": {0, 1, 2, 3},
           "cut": {(k, c) for k in "FB" for c in range(4)}, "sp": {0, 1}, "hv": set(), "k1": {0}, "dzs": False,
-          "wv": {0, 1}}
-COSTS = [{"g": 1.55, "sc": 3.5, "pe": 0.0005, "lat": 0.1, "rl": 2.5, "bw": 60e3},
-         {"g": 1.1, "sc": 5.0, "pe": 0.0005, "lat": 0.15, "rl": 3.5, "bw": 40e3},
-         {"g": 2.0, "sc": 2.5, "pe": 0.0005, "lat": 0.06, "rl": 2.0, "bw": 80e3},
-         {"g": 1.55, "sc": 3.5, "pe": 0.0008, "lat": 0.1, "rl": 3.0, "bw": 50e3}]
-ROUNDS, POLISH, SEED = 1500, 5000, 0
+          "wv": set(), "wc": False}
+COSTS = [{"g": 1.5, "sc": 3.5, "pe": 0.0005, "lat": 0.2, "rl": 2.6, "bw": 60e3, "iss": 0.7, "lb": 250e3},
+         {"g": 1.15, "sc": 4.5, "pe": 0.0005, "lat": 0.25, "rl": 3.2, "bw": 45e3, "iss": 0.9, "lb": 200e3},
+         {"g": 1.9, "sc": 2.5, "pe": 0.0005, "lat": 0.15, "rl": 2.2, "bw": 80e3, "iss": 0.5, "lb": 300e3}]
+ROUNDS, POLISH, SEED = 2500, 8000, 0
 FW = 4096 + 16 * 4
 
 SCRATCH = {
@@ -33,7 +32,7 @@ SCRATCH = {
     "y4": ("sbuf", [128, 16], "int32"), "u1": ("sbuf", [128, 16], "int32"), "c1": ("sbuf", [128, 16], "float32"),
     "c2": ("sbuf", [128, 16], "float32"), "c3": ("sbuf", [128, 16], "float32"),
     "cq": ("sbuf", [128, 128], "bfloat16"), "m32": ("sbuf", [128, 2], "bfloat16"), "idm": ("sbuf", [128, 128], "float32"),
-    "o256": ("sbuf", [128, 128], "bfloat16"),
+    "c8": ("sbuf", [128, 128], "bfloat16"), "o256": ("sbuf", [128, 128], "bfloat16"),
     "arow": ("sbuf", [128, 128], "bfloat16"),
     "hb": ("sbuf", [128, 256], "bfloat16"), "c192": ("sbuf", [128, 128], "bfloat16"), "m192": ("sbuf", [128, 128], "bfloat16"),
     "tni": ("sbuf", [128, 256], "int32"), "lgi": ("sbuf", [128, 256], "int32"), "abi": ("sbuf", [128, 512], "int32"),
@@ -126,7 +125,7 @@ def build(g, T, topo, core, rank, par):
 
     def dma(q, out, in_, rd, wr, nbytes, name="dma"):
         qq = g.sync if q == "Y" else S
-        i = add(q, 0.06, rd, wr, lambda: qq.dma_start(out, in_), lat=1.8 + nbytes / 180e3, kind="d", name=name,
+        i = add(q, 0.06, rd, wr, lambda: qq.dma_start(out, in_), lat=1.6 + nbytes / par["lb"], kind="d", name=name,
                 after=None if rd else prev.get(q))
         prev[q] = i
         ops[i]["sem"] = ("d%d" % cnt["d"], 16)
@@ -146,7 +145,7 @@ def build(g, T, topo, core, rank, par):
             fn = lambda: g.remote_dma_fused([RemoteDMATransfer(dst_ids=[DstId(rid=rid, pnc=pid)], dma_engine_mask=m,
                                                                remote_sem=T.sem[sem], srcs=srcs, dsts=[dst], alu_op=1)],
                                             local_sem=T.sem.sent)
-        i = add("G", 0.8, rd, [], fn, kind="s", name=name, after=after)
+        i = add("G", par["iss"], rd, [], fn, kind="s", name=name, after=after)
         ops[i]["ne"] = ne
         j = add(None, 0.0, [], [key], None, lat=par["rl"] + nbytes / par["bw"], kind="r", name="arr" + name, after=i)
         ops[j]["sem"] = (sem, ne)
@@ -186,68 +185,67 @@ def build(g, T, topo, core, rank, par):
     ts(T.coli[:, 2:3], T.coli[:, 0:1], 15, A_.bitwise_and, ["coli0"], ["coli2"], 1)
     cp(GC, T.coli[:, 1:2], ["coli1"], ["GC"], 1)
     cp(JC, T.coli[:, 2:3], ["coli2"], ["JC"], 1)
-    ts(G15, T.coli[:, 1:2], 16.0, A_.mult, ["coli1"], ["G15"], 1, 15.0, A_.add)
-    ts(P1, T.coli[:, 0:1], 1.0, A_.add, ["coli0"], ["P1"], 1)
+    def aff(out, in_, scale, bias, rd, wr, n, bank=()):
+        return act(out, in_, ACT.Identity, rd, wr, n, bias=bias, scale=scale, bank=bank)
+    iota(T.onb[:], [[0, 256]], 1, 0, ["onb"], 256)
+    aff(G15, GC, 16.0, 15.0, ["GC"], ["G15"], 1)
+    aff(P1, PC, 1.0, 1.0, ["PC"], ["P1"], 1)
     ts(N15, T.coli[:, 2:3], 15.0, A_.is_equal, ["coli2"], ["N15"], 1, -1.0, A_.mult)
     ts(N256, T.coli[:, 2:3], 15.0, A_.not_equal, ["coli2"], ["N256"], 1, -256.0, A_.mult)
-    ts(P16, T.coli[:, 0:1], 16.0, A_.mult, ["coli0"], ["P16"], 1)
-    ts(P1615, T.coli[:, 0:1], 16.0, A_.mult, ["coli0"], ["P1615"], 1, 15.0, A_.add)
-    ts(J32, T.coli[:, 2:3], 32.0, A_.mult, ["coli2"], ["J32"], 1)
-    ts(J16, T.coli[:, 2:3], 16.0, A_.mult, ["coli2"], ["J16"], 1)
-    ts(J2, T.coli[:, 2:3], 4.0, A_.mult, ["coli2"], ["J2"], 1)
+    aff(P16, PC, 16.0, 0.0, ["PC"], ["P16"], 1)
+    aff(P1615, PC, 16.0, 15.0, ["PC"], ["P1615"], 1)
+    aff(J32, JC, 32.0, 0.0, ["JC"], ["J32"], 1)
+    aff(J16, JC, 16.0, float(ROT), ["JC"], ["J16"], 1)
+    aff(J2, JC, 4.0, 0.0, ["JC"], ["J2"], 1)
     ioc = T.ioc[:, 0:128]
-    ts(T.blk[:], T.iog[:], GC, A_.is_equal, ["iog", "GC"], ["blk"], 128)
     ts(T.tm3[:], T.iog[:], GC, A_.is_equal, ["iog", "GC"], ["tm3"], 128, 1.0 / 256, A_.mult)
     add("G", 0.2 + 256 * CY, ["tm3"], ["tri"],
         lambda: g.affine_select(T.tri[:], T.tm3[:], [[1, 128]], A_.is_ge, 0.0, 0, -1), name="tri")
     ts(T.sel8[0:8, :], T.iog[0:8, :], col[0:8, 0:1], A_.is_equal, ["iog", "PC"], ["sel8"], 128, 1.0 / 256, A_.mult)
     ms_(T.c9[0:1, :], 9.0 / 512, ["c9"], 128, 0.5)
-    ms_(T.onb[:], 1.0, ["onb"], 256, 0.5)
-    ms_(T.arow[0:1, :], 0.0, ["arow"], 128, 0.5)
-    ms_(T.m192[:], -192.0, ["m192"], 128, 0.5)
-    ms_(T.m32[0:1, :], 20.0, ["m32"], 2, 0.5)
-    ms_(T.o256[:], 1.0 / 256, ["o256"], 128, 0.5)
+    aff(T.blk[:], T.tm3[:], 256.0, 0.0, ["tm3"], ["blk"], 128)
+    aff(T.arow[0:1, :], T.ioj[0:1, :], 0.0, 0.0, ["ioj"], ["arow"], 128)
+    aff(T.m192[:], T.ioj[:], 0.0, -192.0, ["ioj"], ["m192"], 128)
+    aff(T.m32[0:1, :], T.ioj[0:1, 0:2], 0.0, 20.0, ["ioj"], ["m32"], 2)
+    aff(T.o256[:], T.ioj[:], 0.0, 1.0 / 256, ["ioj"], ["o256"], 128)
     iota(T.iot[0:2, 0:128], [[0, 128]], 12288, -12255, ["iot0"], 128)
-    ts(T.c192[0:2, :], T.iot[0:2, 0:128], 1.0 / 64, A_.mult, ["iot0"], ["c192"], 128)
-    ts(T.idb[:], ioc, PC, A_.is_equal, ["ioc", "PC"], ["idb"], 128)
-    ts(T.idn[:], ioc, PC, A_.is_equal, ["ioc", "PC"], ["idn"], 128, -1.0, A_.mult)
+    aff(T.c192[0:2, :], T.iot[0:2, 0:128], 1.0 / 64, 0.0, ["iot0"], ["c192"], 128)
     ts(T.idf[:], ioc, PC, A_.is_equal, ["ioc", "PC"], ["idf"], 128)
-    if par["dzs"]:
-        ts(T.idm[:], ioc, PC, A_.is_equal, ["ioc", "PC"], ["idm"], 128, -1.0, A_.mult)
-    ts(T.tm1[:], T.iog[:], GC, A_.is_equal, ["iog", "GC", "N15"], ["tm1"], 128, N15, A_.mult)
-    tt(T.Dm[:], T.tm1[:], T.idf[:], A_.add, ["tm1", "idf"], ["Dm"], 128)
+    aff(T.idb[:], T.idf[:], 1.0, 0.0, ["idf"], ["idb"], 128)
+    aff(T.idn[:], T.idf[:], -1.0, 0.0, ["idf"], ["idn"], 128)
+    ts(T.idm[:], T.iog[:], GC, A_.is_equal, ["iog", "GC", "N15"], ["idm"], 128, N15, A_.mult)
+    tt(T.Dm[:], T.idm[:], T.idf[:], A_.add, ["idm", "idf"], ["Dm"], 128)
     ts(T.tm2[:], ioc, P1, A_.is_equal, ["ioc", "P1", "N256"], ["tm2"], 128, N256, A_.mult)
-    ts(T.tm1[:], ioc, PC, A_.is_equal, ["ioc", "PC"], ["tm1"], 128, 256.0, A_.mult)
+    aff(T.tm1[:], T.idf[:], 256.0, 0.0, ["idf"], ["tm1"], 128)
     tt(T.Dd[:], T.tm1[:], T.tm2[:], A_.add, ["tm1", "tm2"], ["Dd"], 128)
     ts(T.sel0[0:8, :], T.ioc[0:8, 0:128], col[0:8, 7:8], A_.is_equal, ["ioc", "P16"], ["sel0"], 128, -1.0, A_.mult)
     ts(T.e8[0:8, :], T.ioc[0:8, :], col[0:8, 8:9], A_.is_equal, ["ioc", "P1615"], ["e8"], 144)
     ts(T.c45[0:1, :], T.ioj[0:1, :], 0.0, A_.is_equal, ["ioj"], ["c45"], 128, -4.5, A_.mult)
     ts(T.Zpos[:], T.ioc[:], G15, A_.is_equal, ["ioc", "G15"], ["Zpos"], 144, 4096.0, A_.mult)
-    ts(T.Zneg[:], T.ioc[:], G15, A_.is_equal, ["ioc", "G15"], ["Zneg"], 144, -4096.0, A_.mult)
-    ts(WC, T.wti[:], 2.0, A_.mult, ["wti"], ["WC"], 1)
-    cp(T.wb[:, 0:1], WC, ["WC"], ["wb"], 1)
-    ts(T.ZW[:], T.ioc[:], G15, A_.is_equal, ["ioc", "G15", "WC"], ["ZW"], 144, WC, A_.mult)
+    aff(T.Zneg[:], T.Zpos[:], -1.0, 0.0, ["Zpos"], ["Zneg"], 144)
+    ts(WC, T.wti[:], 2.0 / 4096, A_.mult, ["wti"], ["WC"], 1)
+    aff(T.wb[:, 0:1], WC, 4096.0, 0.0, ["WC"], ["wb"], 1)
+    aff(T.ZW[:], T.Zpos[:], WC, 0.0, ["Zpos", "WC"], ["ZW"], 144)
     mm([(T.pu[:, 64:65], T.blk[:], T.wb[:, 0:1], True, True, 64)], ["blk", "wb"], ["pu_cw"], "pu")
-    ts(CW, T.pu[:, 64:65], 255.0, A_.mult, ["pu_cw"], ["CW"], 1, bank=["pu"])
+    aff(CW, T.pu[:, 64:65], 255.0, 0.0, ["pu_cw"], ["CW"], 1, ["pu"])
     iota(T.iot[:, 0:128], [[512, 8], [0, 16]], 0, 0, ["iot0"], 128)
-    ts(T.kh[:], T.iot[:, 0:128], J32, A_.add, ["iot0", "J32"], ["kh"], 128)
-    ts(T.kl[:], T.ioj[:], 2.0, A_.mult, ["ioj"], ["kl"], 128)
+    aff(T.kh[:], T.iot[:, 0:128], 1.0, J32, ["iot0", "J32"], ["kh"], 128)
+    aff(T.kl[:], T.ioj[:], 2.0, 0.0, ["ioj"], ["kl"], 128)
     ts(T.rst[:], T.ioj[:], 0.0, A_.is_equal, ["ioj"], ["rst"], 128, 33554432.0, A_.mult)
     iota(T.iot[:, 128:160], [[1, 16], [100, 2]], 0, 0, ["iot1"], 32)
     ts(T.M1[:], T.iot[:, 128:160], JC, A_.is_le, ["iot1", "JC"], ["M1"], 32)
     ts(T.M2[:], T.iot[:, 128:160], -100.0, A_.add, ["iot1", "JC"], ["M2"], 32, JC, A_.is_ge)
-    ts(T.M3[:], T.M2[:], 1.0 / 64, A_.mult, ["M2"], ["M3"], 32)
-    ts(T.rbase[:], T.ioc[:, 0:16], 256.0, A_.mult, ["ioc", "J16"], ["rbase"], 16, J16, A_.add)
-    ts(T.rbase[:], T.rbase[:], float(ROT), A_.add, ["rbase"], ["rbase"], 16)
-    ts(T.cbase[:], T.ioc[:, 0:16], 64.0, A_.mult, ["ioc", "J2"], ["cbase"], 16, J2, A_.add)
+    aff(T.M3[:], T.M2[:], 1.0 / 64, 0.0, ["M2"], ["M3"], 32)
+    aff(T.rbase[:], T.ioc[:, 0:16], 256.0, J16, ["ioc", "J16"], ["rbase"], 16)
+    aff(T.cbase[:], T.ioc[:, 0:16], 64.0, J2, ["ioc", "J2"], ["cbase"], 16)
     nmax = 16 * max(c["n"] for c in chunks)
-    ms_(T.pmask[:, 0:nmax], 1.0, ["pmask"], nmax, 0.5)
-    ms_(T.pmask[:, 15:nmax:16], 0.0, ["pmask"], nmax // 16, 0.5)
+    iota(T.pmask[:, 0:nmax], [[0, nmax]], 1, 0, ["pmask"], nmax)
+    iota(T.pmask[:, 15:nmax:16], [[0, nmax // 16]], 0, 0, ["pmask"], nmax // 16)
     for ci, c in enumerate(chunks):
-        ms_(T.PX[:, c["pos"]:c["pos"] + 1], 0.0, ["PX0%d" % ci], 1)
+        iota(T.PX[:, c["pos"]:c["pos"] + 1], [[0, 1]], 0, 0, ["PX0%d" % ci], 1)
     for gi, G in enumerate(grp):
-        ms_(T.F[:, G["pos"] - 1:G["pos"]], 0.0, ["Fpad%d" % gi], 1)
-        ms_(T.B[:, G["pos"] - 1:G["pos"]], 0.0, ["Bpad%d" % gi], 1)
+        iota(T.F[:, G["pos"] - 1:G["pos"]], [[0, 1]], 0, 0, ["Fpad%d" % gi], 1)
+        iota(T.B[:, G["pos"] - 1:G["pos"]], [[0, 1]], 0, 0, ["Bpad%d" % gi], 1)
 
     def stn(v, G):
         return T["st%d" % v][:, 2 * G["t0"]:2 * G["t0"] + G["n"]]
@@ -256,8 +254,8 @@ def build(g, T, topo, core, rank, par):
         return T["st%d" % v][:, 2 * G["t0"] + G["n"]:2 * G["t1"]]
 
     cp(T.tnb[:], T.tni[:], ["tni"], ["tnb"], 256)
-    cp(T.abb[0:8, 0:256], T.abi[0:8, 0:256], ["ai"], ["ab"], 256)
-    cp(T.abb[0:8, 256:512], T.abi[0:8, 256:512], ["bi"], ["bb"], 256)
+    cp(T.abb[0:8, 0:256], T.abi[0:8, 0:256], ["ai"], ["ab"], 256, name="ab")
+    cp(T.abb[0:8, 256:512], T.abi[0:8, 256:512], ["bi"], ["bb"], 256, name="bb")
     mm([(T.pb[:, 0:256], T.c9[0:1, :], T.onb[0:1, :], True, False, 256),
         (T.pb[:, 0:256], T.sel8[0:8, :], T.abb[0:8, 0:256], False, False, 256),
         (T.pb[:, 0:256], T.tri[:], T.tnb[:], False, True, 256)], ["c9", "onb", "sel8", "ab", "tri", "tnb"],
@@ -270,7 +268,7 @@ def build(g, T, topo, core, rank, par):
     sb0 = T.sb0
     mm([(T.pk1[:, 0:256], T.sel8[0:8, :], T.abb[0:8, 256:512], True, True, 256)], ["sel8", "bb"], ["pk1"], "pk1")
     act(sb0[:, 768:1024], T.pk1[:, 0:256], ACT.Identity, ["pk1"], ["sb0b"], 256, bias=-255.0 / 512, bank=["pk1"])
-    ts(sb0[:, 0:256], T.spb[:], -1.0, A_.mult, ["spb"], ["sb0s"], 256, 255.0, A_.add, 0.5)
+    aff(sb0[:, 0:256], T.spb[:], -1.0, 255.0, ["spb"], ["sb0s"], 256)
     lst = [(T.pk0[:, 0:256], T.idb[:], T.spb[:], True, False, 256), (T.pk0[:, 0:256], T.idn[:], T.epb[:], False, False, 256)]
     for c in chunks:
         o = T.pk0[:, c["t0"] + 1:c["t1"]]
@@ -282,7 +280,7 @@ def build(g, T, topo, core, rank, par):
     cp(T.thf[0:8, :], T.thi[0:8, :], ["thi"], ["thf"], 256)
     mm([(T.pm[:, 0:16], T.e8[0:8, 15 - r:143 - r], T.thf[0:8, r:256:16], r == 0, r == 15, 256) for r in range(16)],
        ["e8", "thf"], ["pm"], "pm")
-    ts(T.thk[:], T.pm[:, 0:16], 4096.0, A_.mult, ["pm"], ["thk"], 16, 4095.0, A_.add, bank=["pm"])
+    aff(T.thk[:], T.pm[:, 0:16], 4096.0, 4095.0, ["pm"], ["thk"], 16, ["pm"])
     iota(T.cn[:, 0:1024:2], [[0, 512]], 0, 0, ["cn"], 512)
     ts(T.cn[:, 1:1024:2], T.cti[:], 64.0, A_.mult, ["cti"], ["cn"], 512, 9472.0625, A_.add)
 
@@ -312,8 +310,11 @@ def build(g, T, topo, core, rank, par):
             G["kn"], G["kw"] = kn, kw
             bk = ("pb", "pw")[gi & 1]
             pa, pz, kz = T[bk][:, 256 + G["t0"]:256 + G["t1"]], T[bk][:, sl], ["pb%d" % gi]
-            mm([(pa, T.idf[:], stw(v, G), True, True, 4 * n)], ["idf"] + kw, ["pw%d" % gi], bk, "wcopy")
-            tt(T.rf[:, sl], stn(v, G), pa, A_.mult, kn + ["pw%d" % gi], ["rf%d" % gi], n, 1.0, [bk], "prodF")
+            if par["wc"]:
+                mm([(pa, T.idf[:], stw(v, G), True, True, 4 * n)], ["idf"] + kw, ["pw%d" % gi], bk, "wcopy")
+                tt(T.rf[:, sl], stn(v, G), pa, A_.mult, kn + ["pw%d" % gi], ["rf%d" % gi], n, 1.0, [bk], "prodF")
+            else:
+                tt(T.rf[:, sl], stn(v, G), stw(v, G), A_.mult, kn + kw, ["rf%d" % gi], n, 2.0, name="prodF")
             ts(T.rf[:, sl], T.rf[:, sl], 4095, A_.bitwise_and, ["rf%d" % gi], ["rf%d" % gi], n, name="andF")
             cp(lf[:, sl], T.rf[:, sl], ["rf%d" % gi], ["lf%d_%d" % (v & 1, gi)], n, name="u16F")
             bs, ka = sb[:, 768 + G["t0"]:768 + G["t1"]], ["pw%d" % gi]
@@ -342,8 +343,11 @@ def build(g, T, topo, core, rank, par):
             cp(T.lb[:, sl], T.rb[:, sl], ["rb%d" % gi], ["lb%d" % gi], n, name="u16B")
             dzo = T.db[:, 2 * G["t0"] + n:2 * G["t1"]]
             if par["dzs"]:
-                mm([(pz, T.idm[:], stw(v, G), False, True, 4 * n)], ["idm"] + kw, kz, bk, "dzm")
-                act(dzo, pz, ACT.Identity, kz, ["dz%d" % gi], n, bank=[bk], name="dz")
+                mm([(pa, T.idm[:], stw(v, G), True, False, 4 * n), (pa, T.idb[:], bs, False, False, n),
+                    (pa, T.arow[0:1, :], T.onb[0:1, 0:n], False, False, n), (pa, T.c192[0:2, :], T.onb[0:2, 0:n], False, False, n),
+                    (pa, T.idn[:], T.hb[:, sl], False, True, n)],
+                   ["idm", "idb", "arow", "c192", "onb", "idn", "hb%d" % gi] + kw + kB, ka, bk, "dzm")
+                act(dzo, pa, ACT.Identity, ka, ["dz%d" % gi], n, bank=[bk], name="dz")
             else:
                 tt(dzo, pz, stw(v, G), A_.subtract, kz + kw, ["dz%d" % gi], n, 1.0, [bk], "dz")
         mm([(T.pu[:, 0:16], T.ZW[:, 15 - r:143 - r], sb[:, r:256:16], r == 0, r == 15, 64) for r in range(16)],
@@ -441,9 +445,7 @@ def build(g, T, topo, core, rank, par):
                 tt(T.cd[:, qs], T.k2[:, qs], T.nok[:, qs], A_.add, ["k2" + s, "nok" + s], ["cd" + s], Q, name="cd")
             cp(T.l2[:, qs], T.cd[:, qs], ["cd" + s], ["l2" + s], Q, name="l2")
             if not last:
-                mm([(T.pm[0:1, 0:128], T.m32[0:1, 0:1], T.onb[0:1, 0:128], True, False, 128)][:1 if gi == 0 else 0]
-                   + [(T.pm[0:1, 0:128], T.nok[:, q:q + 1], T.o256[:], False, q == 15, 128) for q in range(G["q0"], G["q1"])],
-                   ["nok" + s, "onb", "o256", "m32"], ["pm"], "pm", "count")
+                mm([(T.pm[0:Q, 128:256], T.nok[:, qs], T.o256[:], gi == 0, gi == NG - 1, 128)], ["nok" + s, "o256"], ["pm8"], "pm", "count")
             PXall = [k % ci for ci in G["cs"] for k in ("PX%d", "PX0%d")]
             tt(T.mp[:, sl], T.PX[:, p:e].indirect(T.l1[:, qs]), sb[:, sl], A_.min, PXall + ["l1" + s] + kS, ["mp" + s], n, gc_, name="mp")
             uo = T.pu[:, 16 + G["q0"]:16 + G["q1"]]
@@ -493,6 +495,10 @@ def build(g, T, topo, core, rank, par):
                              G["kn"] + G["kw"] + ["ez%d_%d" % (v, gi), "el%d_%d" % (v, gi)], "st%d_%d" % (v + 1, gi), 1024 * n,
                              "dyn%d_%d" % (v, gi), last_send)
         if not last:
+            Q = grp[0]["q1"]
+            act(T.c8[0:Q, :], T.pm[0:Q, 128:256], ACT.Identity, ["pm8"], ["c8"], 128, bank=["pm"], name="c8")
+            mm([(T.pm[0:1, 0:128], T.m32[0:1, 0:1], T.onb[0:1, 0:128], True, False, 128),
+                (T.pm[0:1, 0:128], T.onb[0:Q, 0:1], T.c8[0:Q, :], False, True, 128)], ["m32", "onb", "c8"], ["pm"], "pm", "csum")
             act(T.cq[0:1, :], T.pm[0:1, 0:128], ACT.Identity, ["pm"], ["cq"], 128, bias=-15.5 / 256, bank=["pm"], name="cq")
             tt(T.arow[0:1, :], T.pm[0:1, 0:128], T.cq[0:1, :], A_.subtract, ["pm", "cq"], ["arow"], 128, 1.0, ["pm"], "arow")
         for gi, G in enumerate(grp):
@@ -665,14 +671,17 @@ def improve(variants, lat, rounds, seed):
     best, cur, bkey, border = 1e9, 1e9, key, None
     tag = np.array([o["name"] for o in ops])
     names = sorted(set(tag.tolist()))
-    starts = [i for i in range(n) if ops[i]["name"] == "wcopy" and ops[i - 1]["name"] != "dz"]
+    starts = [i for i in range(1, n) if ops[i - 1]["at"][0] >= 0 and (i < 2 or ops[i - 2]["at"][0] != ops[i - 1]["at"][0])]
     per = starts[2] - starts[1]
     for it in range(rounds):
         passes = 0
         if it:
             k = np.array(bkey)
-            mode = int(rng.integers(0, 4))
-            if mode == 0:
+            mode = int(rng.integers(0, 5))
+            if mode == 4:
+                a, b = [starts[int(x)] - 1 for x in rng.choice(3, 2, replace=False)]
+                k[b:b + per] = k[a:a + per] + float(np.median(k[b:b + per] - k[a:a + per]))
+            elif mode == 0:
                 k = k + rng.normal(0.0, float(rng.choice([0.1, 0.3, 1.0])), n) * (rng.random(n) < 0.2)
             elif mode == 1:
                 for nm in rng.choice(names, int(rng.integers(1, 5))):

import numpy as np
from concourse.bass import DstId, RemoteDMATransfer
from concourse.mybir import AluOpType, ActivationFunctionType

NV, STEP, ROT = 4, 3, 167
CHOICE = {"groups": [[64, 64], [64, 64]], "gv": {("B", 0)}, "zs": {3}, "ab": {2}, "ev": {0, 1, 2, 3},
          "cut": {(k, c) for k in "FB" for c in range(4)}, "sp": {0, 1}, "hv": set(), "k1": {0}, "dzs": False,
          "wv": set(), "wc": False}
COSTS = [{"g": 1.5, "sc": 3.5, "pe": 0.0005, "lat": 0.2, "rl": 2.6, "bw": 60e3, "iss": 0.7, "lb": 250e3},
         {"g": 1.15, "sc": 4.5, "pe": 0.0005, "lat": 0.25, "rl": 3.2, "bw": 45e3, "iss": 0.9, "lb": 200e3},
         {"g": 1.9, "sc": 2.5, "pe": 0.0005, "lat": 0.15, "rl": 2.2, "bw": 80e3, "iss": 0.5, "lb": 300e3}]
ROUNDS, POLISH, SEED = 2500, 8000, 0
FW = 4096 + 16 * 4

SCRATCH = {
    "x": ("sbuf", [128, 4272], "bfloat16"),
    "F": ("sbuf", [128, FW], "bfloat16"), "B": ("sbuf", [128, FW], "bfloat16"),
    "PX": ("sbuf", [128, FW], "bfloat16"), "Y": ("sbuf", [128, FW], "bfloat16"),
    "Zp": ("sbuf", [128, 16, 16, 16], "bfloat16"), "Zn": ("sbuf", [128, 16, 16, 16], "bfloat16"),
    "pmask": ("sbuf", [128, 2048], "bfloat16"),
    "cn": ("sbuf", [128, 1024], "float32"), "db": ("sbuf", [128, 512], "float32"),
    "lf0": ("sbuf", [128, 256], "uint16"), "lf1": ("sbuf", [128, 256], "uint16"), "lb": ("sbuf", [128, 256], "uint16"),
    "l1": ("sbuf", [128, 16], "uint16"), "l2": ("sbuf", [128, 16], "uint16"), "l3": ("sbuf", [128, 16], "uint16"),
    "l4": ("sbuf", [128, 16], "uint16"), "l5": ("sbuf", [128, 16], "uint16"),
    "rf": ("sbuf", [128, 256], "int32"), "rb": ("sbuf", [128, 256], "int32"), "hh": ("sbuf", [128, 256], "int32"),
    "svF": ("sbuf", [128, 256], "bfloat16"), "svB": ("sbuf", [128, 256], "bfloat16"),
    "ms": ("sbuf", [128, 256], "float32"), "mp": ("sbuf", [128, 256], "bfloat16"),
    "fk": ("sbuf", [128, 256], "bfloat16"), "fb": ("sbuf", [128, 256], "bfloat16"), "av": ("sbuf", [128, 256], "bfloat16"),
    "ki": ("sbuf", [128, 16], "int32"), "of": ("sbuf", [128, 16], "int32"), "k2": ("sbuf", [128, 16], "int32"),
    "cd": ("sbuf", [128, 16], "int32"), "nok": ("sbuf", [128, 16], "bfloat16"), "us": ("sbuf", [128, 16], "float32"),
    "ui": ("sbuf", [128, 16], "int32"), "u9": ("sbuf", [128, 16], "int32"), "u4": ("sbuf", [128, 16], "int32"),
    "y4": ("sbuf", [128, 16], "int32"), "u1": ("sbuf", [128, 16], "int32"), "c1": ("sbuf", [128, 16], "float32"),
    "c2": ("sbuf", [128, 16], "float32"), "c3": ("sbuf", [128, 16], "float32"),
    "cq": ("sbuf", [128, 128], "bfloat16"), "m32": ("sbuf", [128, 2], "bfloat16"), "idm": ("sbuf", [128, 128], "float32"),
    "c8": ("sbuf", [128, 128], "bfloat16"), "o256": ("sbuf", [128, 128], "bfloat16"),
    "arow": ("sbuf", [128, 128], "bfloat16"),
    "hb": ("sbuf", [128, 256], "bfloat16"), "c192": ("sbuf", [128, 128], "bfloat16"), "m192": ("sbuf", [128, 128], "bfloat16"),
    "tni": ("sbuf", [128, 256], "int32"), "lgi": ("sbuf", [128, 256], "int32"), "abi": ("sbuf", [128, 512], "int32"),
    "spb": ("sbuf", [128, 256], "bfloat16"), "epb": ("sbuf", [128, 256], "bfloat16"), "wti": ("sbuf", [128, 1], "int32"),
    "thi": ("sbuf", [128, 256], "int32"), "cti": ("sbuf", [128, 512], "int32"),
    "tnb": ("sbuf", [128, 256], "bfloat16"), "abb": ("sbuf", [128, 512], "bfloat16"), "thf": ("sbuf", [128, 256], "float32"),
    "thk": ("sbuf", [128, 16], "float32"), "col": ("sbuf", [128, 16], "float32"), "coli": ("sbuf", [128, 4], "int32"),
    "wb": ("sbuf", [128, 2], "bfloat16"),
    "ioc": ("sbuf", [128, 144], "float32"), "iog": ("sbuf", [128, 128], "float32"), "ioj": ("sbuf", [128, 128], "float32"),
    "iot": ("sbuf", [128, 256], "float32"),
    "idb": ("sbuf", [128, 128], "bfloat16"), "idn": ("sbuf", [128, 128], "bfloat16"), "idf": ("sbuf", [128, 128], "float32"),
    "Dm": ("sbuf", [128, 128], "float32"), "Dd": ("sbuf", [128, 128], "float32"), "tm1": ("sbuf", [128, 128], "float32"),
    "tm2": ("sbuf", [128, 128], "float32"), "tm3": ("sbuf", [128, 128], "float32"),
    "blk": ("sbuf", [128, 128], "bfloat16"), "tri": ("sbuf", [128, 128], "bfloat16"),
    "sel8": ("sbuf", [128, 128], "bfloat16"), "sel0": ("sbuf", [128, 128], "bfloat16"), "e8": ("sbuf", [128, 144], "float32"),
    "c45": ("sbuf", [128, 128], "bfloat16"), "c9": ("sbuf", [128, 128], "bfloat16"),
    "Zpos": ("sbuf", [128, 144], "bfloat16"), "Zneg": ("sbuf", [128, 144], "bfloat16"), "ZW": ("sbuf", [128, 144], "bfloat16"),
    "kh": ("sbuf", [128, 128], "bfloat16"), "kl": ("sbuf", [128, 128], "bfloat16"), "rst": ("sbuf", [128, 128], "float32"),
    "M3": ("sbuf", [128, 32], "float32"), "M1": ("sbuf", [128, 32], "float32"), "M2": ("sbuf", [128, 32], "float32"),
    "rbase": ("sbuf", [128, 16], "float32"), "cbase": ("sbuf", [128, 16], "float32"),
    "onb": ("sbuf", [128, 256], "bfloat16"), "onf": ("sbuf", [128, 128], "float32"),
    "oL": ("sbuf", [128, 256], "float32"), "oT": ("sbuf", [128, 256], "float32"), "ng": ("sbuf", [128, 256], "float32"),
    "oC": ("sbuf", [128, 512], "float32"),
}
for _v in range(NV + 1):
    SCRATCH["st%d" % _v] = ("sbuf", [128, 512], "float32")
for _v in range(NV):
    SCRATCH["sb%d" % _v] = ("sbuf", [128, 1024], "bfloat16")
    SCRATCH["eb%d" % _v] = ("sbuf", [128, 512], "float32")
for _n in ("pc0", "pc1", "pk0", "pk1", "pu", "pw", "pb", "pm"):
    SCRATCH[_n] = ("psum", [128, 512], "float32")
SEMAPHORES = ["cV", "cS", "cP", "cG", "sent"] + ["d%d" % i for i in range(40)] + ["r%d" % i for i in range(24)]

CY = 0.00083 * 1.2
A_ = AluOpType
ACT = ActivationFunctionType


def build(g, T, topo, core, rank, par):
    ops = []
    cnt = {"d": 0, "r": 0}
    prev = {}
    ctx = {"v": -1, "g": 0, "c": 0}
    V, S, P = g.vector, g.scalar, g.tensor

    def add(eng, dur, rd, wr, fn, bank=(), lat=0.0, kind="c", name="", after=None):
        ops.append({"at": (ctx["v"], ctx["g"], ctx["c"]), "eng": eng, "dur": dur, "rd": list(rd), "wr": list(wr), "fn": fn, "bank": list(bank), "lat": lat,
                    "kind": kind, "name": name, "after": after, "sem": None})
        return len(ops) - 1

    def vc(n, c=1.0):
        return max(64.0, n * c) * CY + 0.02

    def ts(out, in0, s1, op0, rd, wr, n, s2=None, op1=None, c=1.0, bank=(), name="ts"):
        if op1 is None:
            fn = lambda: V.tensor_scalar(out, in0, s1, None, op0)
        else:
            fn = lambda: V.tensor_scalar(out, in0, s1, s2, op0, op1)
        return add("V", vc(n, c), rd, wr, fn, bank, name=name)

    def tt(out, in0, in1, op, rd, wr, n, c=2.0, bank=(), name="tt"):
        return add("V", vc(n, c), rd, wr, lambda: V.tensor_tensor(out, in0, in1, op), bank, name=name)

    def cp(out, in_, rd, wr, n, c=1.0, bank=(), name="cp"):
        return add("V", vc(n, c), rd, wr, lambda: V.tensor_copy(out, in_), bank, name=name)

    def ms_(out, val, wr, n, c=1.0):
        return add("V", vc(n, c), [], wr, lambda: V.memset(out, val), name="memset")

    def act(out, in_, func, rd, wr, n, bias=0.0, scale=1.0, c=1.0, bank=(), name="act"):
        return add("S", vc(n, c) + 0.03, rd, wr, lambda: S.activation(out, in_, func, bias=bias, scale=scale), bank, name=name)

    def mm(lst, rd, wr, bank, name="mm"):
        def fn():
            last = None
            for o, l, r, s0, s1, _c in lst:
                last = P.matmul(o, l, r, s0, s1)
            return last
        return add("P", sum(m[5] for m in lst) * par["pe"] + 0.03, rd, wr, fn, [bank], name=name)

    def iota(out, pat, base, cm, wr, n, flt=True):
        if flt:
            fn = lambda: g.iota(out, pat, base, cm, allow_small_or_imprecise_dtypes=True)
        else:
            fn = lambda: g.iota(out, pat, base, cm)
        return add("G", 0.156 + 2 * n * CY, [], wr, fn, name="iota")

    def gcp(out, in_, rd, wr, n, name="gcp"):
        return add("G", 0.2 + 2 * n * CY, rd, wr, lambda: g.affine_select(out, in_, [[0, n]], A_.is_ge, 0.0, 0, 0), name=name)

    def dma(q, out, in_, rd, wr, nbytes, name="dma"):
        qq = g.sync if q == "Y" else S
        i = add(q, 0.06, rd, wr, lambda: qq.dma_start(out, in_), lat=1.6 + nbytes / par["lb"], kind="d", name=name,
                after=None if rd else prev.get(q))
        prev[q] = i
        ops[i]["sem"] = ("d%d" % cnt["d"], 16)
        cnt["d"] += 1
        return i

    def send(dst_rank, srcs, dst, rd, key, nbytes, name, after=None):
        dc = T.cores[dst_rank]
        rid, pid, _e = topo.addr(dc)
        m = topo.mask(core, dc)
        ne = len(topo.engines(core, dc))
        sem = "r%d" % cnt["r"]
        cnt["r"] += 1
        if len(srcs) == 1:
            fn = lambda: g.remote_dma(dst, srcs[0], T.sem[sem], T.sem.sent, pid, rid, m)
        else:
            fn = lambda: g.remote_dma_fused([RemoteDMATransfer(dst_ids=[DstId(rid=rid, pnc=pid)], dma_engine_mask=m,
                                                               remote_sem=T.sem[sem], srcs=srcs, dsts=[dst], alu_op=1)],
                                            local_sem=T.sem.sent)
        i = add("G", par["iss"], rd, [], fn, kind="s", name=name, after=after)
        ops[i]["ne"] = ne
        j = add(None, 0.0, [], [key], None, lat=par["rl"] + nbytes / par["bw"], kind="r", name="arr" + name, after=i)
        ops[j]["sem"] = (sem, ne)
        return i

    grp, chunks, t = [], [], 0
    for gi, sizes in enumerate(par["groups"]):
        g0 = t
        cs = []
        for n in sizes:
            cs.append(len(chunks))
            chunks.append({"g": gi, "t0": t, "t1": t + n, "n": n, "pos": 16 * (gi + 1) + 16 * t, "first": t == g0})
            t += n
        grp.append({"t0": g0, "t1": t, "n": t - g0, "pos": 16 * (gi + 1) + 16 * g0, "cs": cs, "q0": g0 // 16, "q1": t // 16})
    NG = len(grp)
    col = T.col
    PC, JC, GC, G15, P1, N15, N256, P16, P1615, J32, J16, J2, WC, CW = [col[:, i:i + 1] for i in range(14)]

    dma("Y", T.tni[:], T.tn[:], [], ["tni"], 131072)
    dma("S", T.abi[0:8, 0:256], T.aa[:], [], ["ai"], 8192)
    dma("S", T.abi[0:8, 256:512], T.bb[:], [], ["bi"], 8192)
    dma("Y", T.lgi[:], T.lg[:], [], ["lgi"], 131072)
    dma("Y", T.x[:, ROT:4096], T.xt[:, 0:4096 - ROT], [], ["x"], 1350000)
    dma("S", T.x[:, 0:ROT], T.xt[:, 4096 - ROT:4096], [], ["x2"], 50000)
    dma("S", T.spb[:], T.sp[:], [], ["spb"], 500000)
    dma("S", T.epb[:], T.ep[:], [], ["epb"], 600000)
    dma("S", T.wti[:], T.wt[:], [], ["wti"], 50000)
    dma("S", T.thi[0:8, :], T.th[:], [], ["thi"], 50000)
    dma("Y", T.cti[:], T.ct[:], [], ["cti"], 1650000)

    iota(T.coli[:, 0:1], [[0, 1]], 0, 1, ["coli0"], 1, False)
    iota(T.iog[:], [[1, 8], [0, 16]], 0, 0, ["iog"], 128)
    iota(T.ioc[:], [[1, 144]], 0, 0, ["ioc"], 144)
    iota(T.ioj[:], [[0, 8], [1, 16]], 0, 0, ["ioj"], 128)
    cp(PC, T.coli[:, 0:1], ["coli0"], ["PC"], 1)
    ts(T.coli[:, 1:2], T.coli[:, 0:1], 4, A_.arith_shift_right, ["coli0"], ["coli1"], 1)
    ts(T.coli[:, 2:3], T.coli[:, 0:1], 15, A_.bitwise_and, ["coli0"], ["coli2"], 1)
    cp(GC, T.coli[:, 1:2], ["coli1"], ["GC"], 1)
    cp(JC, T.coli[:, 2:3], ["coli2"], ["JC"], 1)
    def aff(out, in_, scale, bias, rd, wr, n, bank=()):
        return act(out, in_, ACT.Identity, rd, wr, n, bias=bias, scale=scale, bank=bank)
    iota(T.onb[:], [[0, 256]], 1, 0, ["onb"], 256)
    aff(G15, GC, 16.0, 15.0, ["GC"], ["G15"], 1)
    aff(P1, PC, 1.0, 1.0, ["PC"], ["P1"], 1)
    ts(N15, T.coli[:, 2:3], 15.0, A_.is_equal, ["coli2"], ["N15"], 1, -1.0, A_.mult)
    ts(N256, T.coli[:, 2:3], 15.0, A_.not_equal, ["coli2"], ["N256"], 1, -256.0, A_.mult)
    aff(P16, PC, 16.0, 0.0, ["PC"], ["P16"], 1)
    aff(P1615, PC, 16.0, 15.0, ["PC"], ["P1615"], 1)
    aff(J32, JC, 32.0, 0.0, ["JC"], ["J32"], 1)
    aff(J16, JC, 16.0, float(ROT), ["JC"], ["J16"], 1)
    aff(J2, JC, 4.0, 0.0, ["JC"], ["J2"], 1)
    ioc = T.ioc[:, 0:128]
    ts(T.tm3[:], T.iog[:], GC, A_.is_equal, ["iog", "GC"], ["tm3"], 128, 1.0 / 256, A_.mult)
    add("G", 0.2 + 256 * CY, ["tm3"], ["tri"],
        lambda: g.affine_select(T.tri[:], T.tm3[:], [[1, 128]], A_.is_ge, 0.0, 0, -1), name="tri")
    ts(T.sel8[0:8, :], T.iog[0:8, :], col[0:8, 0:1], A_.is_equal, ["iog", "PC"], ["sel8"], 128, 1.0 / 256, A_.mult)
    ms_(T.c9[0:1, :], 9.0 / 512, ["c9"], 128, 0.5)
    aff(T.blk[:], T.tm3[:], 256.0, 0.0, ["tm3"], ["blk"], 128)
    aff(T.arow[0:1, :], T.ioj[0:1, :], 0.0, 0.0, ["ioj"], ["arow"], 128)
    aff(T.m192[:], T.ioj[:], 0.0, -192.0, ["ioj"], ["m192"], 128)
    aff(T.m32[0:1, :], T.ioj[0:1, 0:2], 0.0, 20.0, ["ioj"], ["m32"], 2)
    aff(T.o256[:], T.ioj[:], 0.0, 1.0 / 256, ["ioj"], ["o256"], 128)
    iota(T.iot[0:2, 0:128], [[0, 128]], 12288, -12255, ["iot0"], 128)
    aff(T.c192[0:2, :], T.iot[0:2, 0:128], 1.0 / 64, 0.0, ["iot0"], ["c192"], 128)
    ts(T.idf[:], ioc, PC, A_.is_equal, ["ioc", "PC"], ["idf"], 128)
    aff(T.idb[:], T.idf[:], 1.0, 0.0, ["idf"], ["idb"], 128)
    aff(T.idn[:], T.idf[:], -1.0, 0.0, ["idf"], ["idn"], 128)
    ts(T.idm[:], T.iog[:], GC, A_.is_equal, ["iog", "GC", "N15"], ["idm"], 128, N15, A_.mult)
    tt(T.Dm[:], T.idm[:], T.idf[:], A_.add, ["idm", "idf"], ["Dm"], 128)
    ts(T.tm2[:], ioc, P1, A_.is_equal, ["ioc", "P1", "N256"], ["tm2"], 128, N256, A_.mult)
    aff(T.tm1[:], T.idf[:], 256.0, 0.0, ["idf"], ["tm1"], 128)
    tt(T.Dd[:], T.tm1[:], T.tm2[:], A_.add, ["tm1", "tm2"], ["Dd"], 128)
    ts(T.sel0[0:8, :], T.ioc[0:8, 0:128], col[0:8, 7:8], A_.is_equal, ["ioc", "P16"], ["sel0"], 128, -1.0, A_.mult)
    ts(T.e8[0:8, :], T.ioc[0:8, :], col[0:8, 8:9], A_.is_equal, ["ioc", "P1615"], ["e8"], 144)
    ts(T.c45[0:1, :], T.ioj[0:1, :], 0.0, A_.is_equal, ["ioj"], ["c45"], 128, -4.5, A_.mult)
    ts(T.Zpos[:], T.ioc[:], G15, A_.is_equal, ["ioc", "G15"], ["Zpos"], 144, 4096.0, A_.mult)
    aff(T.Zneg[:], T.Zpos[:], -1.0, 0.0, ["Zpos"], ["Zneg"], 144)
    ts(WC, T.wti[:], 2.0 / 4096, A_.mult, ["wti"], ["WC"], 1)
    aff(T.wb[:, 0:1], WC, 4096.0, 0.0, ["WC"], ["wb"], 1)
    aff(T.ZW[:], T.Zpos[:], WC, 0.0, ["Zpos", "WC"], ["ZW"], 144)
    mm([(T.pu[:, 64:65], T.blk[:], T.wb[:, 0:1], True, True, 64)], ["blk", "wb"], ["pu_cw"], "pu")
    aff(CW, T.pu[:, 64:65], 255.0, 0.0, ["pu_cw"], ["CW"], 1, ["pu"])
    iota(T.iot[:, 0:128], [[512, 8], [0, 16]], 0, 0, ["iot0"], 128)
    aff(T.kh[:], T.iot[:, 0:128], 1.0, J32, ["iot0", "J32"], ["kh"], 128)
    aff(T.kl[:], T.ioj[:], 2.0, 0.0, ["ioj"], ["kl"], 128)
    ts(T.rst[:], T.ioj[:], 0.0, A_.is_equal, ["ioj"], ["rst"], 128, 33554432.0, A_.mult)
    iota(T.iot[:, 128:160], [[1, 16], [100, 2]], 0, 0, ["iot1"], 32)
    ts(T.M1[:], T.iot[:, 128:160], JC, A_.is_le, ["iot1", "JC"], ["M1"], 32)
    ts(T.M2[:], T.iot[:, 128:160], -100.0, A_.add, ["iot1", "JC"], ["M2"], 32, JC, A_.is_ge)
    aff(T.M3[:], T.M2[:], 1.0 / 64, 0.0, ["M2"], ["M3"], 32)
    aff(T.rbase[:], T.ioc[:, 0:16], 256.0, J16, ["ioc", "J16"], ["rbase"], 16)
    aff(T.cbase[:], T.ioc[:, 0:16], 64.0, J2, ["ioc", "J2"], ["cbase"], 16)
    nmax = 16 * max(c["n"] for c in chunks)
    iota(T.pmask[:, 0:nmax], [[0, nmax]], 1, 0, ["pmask"], nmax)
    iota(T.pmask[:, 15:nmax:16], [[0, nmax // 16]], 0, 0, ["pmask"], nmax // 16)
    for ci, c in enumerate(chunks):
        iota(T.PX[:, c["pos"]:c["pos"] + 1], [[0, 1]], 0, 0, ["PX0%d" % ci], 1)
    for gi, G in enumerate(grp):
        iota(T.F[:, G["pos"] - 1:G["pos"]], [[0, 1]], 0, 0, ["Fpad%d" % gi], 1)
        iota(T.B[:, G["pos"] - 1:G["pos"]], [[0, 1]], 0, 0, ["Bpad%d" % gi], 1)

    def stn(v, G):
        return T["st%d" % v][:, 2 * G["t0"]:2 * G["t0"] + G["n"]]

    def stw(v, G):
        return T["st%d" % v][:, 2 * G["t0"] + G["n"]:2 * G["t1"]]

    cp(T.tnb[:], T.tni[:], ["tni"], ["tnb"], 256)
    cp(T.abb[0:8, 0:256], T.abi[0:8, 0:256], ["ai"], ["ab"], 256, name="ab")
    cp(T.abb[0:8, 256:512], T.abi[0:8, 256:512], ["bi"], ["bb"], 256, name="bb")
    mm([(T.pb[:, 0:256], T.c9[0:1, :], T.onb[0:1, :], True, False, 256),
        (T.pb[:, 0:256], T.sel8[0:8, :], T.abb[0:8, 0:256], False, False, 256),
        (T.pb[:, 0:256], T.tri[:], T.tnb[:], False, True, 256)], ["c9", "onb", "sel8", "ab", "tri", "tnb"],
       ["pb%d" % i for i in range(NG)], "pb")
    for gi, G in enumerate(grp):
        sl = slice(G["t0"], G["t1"])
        ts(T.hh[:, sl], T.pb[:, sl], -0.515625, A_.add, ["pb%d" % gi], ["hh%d" % gi], G["n"], bank=["pb"])
        tt(stw(0, G), T.pb[:, sl], T.hh[:, sl], A_.subtract, ["pb%d" % gi, "hh%d" % gi], ["st0w%d" % gi], G["n"], 1.0, ["pb"])
        ts(stn(0, G), T.lgi[:, sl], 64.0, A_.mult, ["lgi"], ["st0n%d" % gi], G["n"], 9472.0625, A_.add)
    sb0 = T.sb0
    mm([(T.pk1[:, 0:256], T.sel8[0:8, :], T.abb[0:8, 256:512], True, True, 256)], ["sel8", "bb"], ["pk1"], "pk1")
    act(sb0[:, 768:1024], T.pk1[:, 0:256], ACT.Identity, ["pk1"], ["sb0b"], 256, bias=-255.0 / 512, bank=["pk1"])
    aff(sb0[:, 0:256], T.spb[:], -1.0, 255.0, ["spb"], ["sb0s"], 256)
    lst = [(T.pk0[:, 0:256], T.idb[:], T.spb[:], True, False, 256), (T.pk0[:, 0:256], T.idn[:], T.epb[:], False, False, 256)]
    for c in chunks:
        o = T.pk0[:, c["t0"] + 1:c["t1"]]
        lst.append((o, T.idn[:], T.spb[:, c["t0"]:c["t1"] - 1], False, False, c["n"]))
        lst.append((o, T.idb[:], T.epb[:, c["t0"]:c["t1"] - 1], False, c is chunks[-1], c["n"]))
    mm(lst, ["idb", "idn", "spb", "epb"], ["pk0"], "pk0")
    act(sb0[:, 256:512], T.pk0[:, 0:256], ACT.Identity, ["pk0"], ["sb0h"], 256, bank=["pk0"])
    tt(sb0[:, 512:768], T.pk0[:, 0:256], sb0[:, 256:512], A_.subtract, ["pk0", "sb0h"], ["sb0l"], 256, 1.0, ["pk0"])
    cp(T.thf[0:8, :], T.thi[0:8, :], ["thi"], ["thf"], 256)
    mm([(T.pm[:, 0:16], T.e8[0:8, 15 - r:143 - r], T.thf[0:8, r:256:16], r == 0, r == 15, 256) for r in range(16)],
       ["e8", "thf"], ["pm"], "pm")
    aff(T.thk[:], T.pm[:, 0:16], 4096.0, 4095.0, ["pm"], ["thk"], 16, ["pm"])
    iota(T.cn[:, 0:1024:2], [[0, 512]], 0, 0, ["cn"], 512)
    ts(T.cn[:, 1:1024:2], T.cti[:], 64.0, A_.mult, ["cti"], ["cn"], 512, 9472.0625, A_.add)

    gc_, sc_ = par["g"], par["sc"]
    last_send = None
    nr = len(T.cores)
    for v in range(NV):
        last = v == NV - 1
        ctx.update({"v": v, "g": 0, "c": 0})
        sb = T["sb%d" % v]
        kS, kH, kL, kB = (["sb0s"], ["sb0h"], ["sb0l"], ["sb0b"]) if v == 0 else (["sb%d" % v],) * 4
        lf = T["lf%d" % (v & 1)]
        eb = T["eb%d" % v]
        XK = ["x", "x2"]
        if not last:
            last_send = send((rank + STEP) % nr, [sb[:]], T["sb%d" % (v + 1)][:], kS + kH + kL + kB, "sb%d" % (v + 1), 262144,
                             "stat%d" % v, last_send)
        else:
            gcp(T.x[:, 4096:4096 + ROT], T.x[:, 0:ROT], XK + ["xg"], ["xw"], ROT)
            XK = XK + ["xg"]
        for gi, G in enumerate(grp):
            n, sl = G["n"], slice(G["t0"], G["t1"])
            kn, kw = (["st0n%d" % gi], ["st0w%d" % gi]) if v == 0 else (["st%d_%d" % (v, gi)],) * 2
            if v and gi in par["sp"]:
                kn = ["sn%d_%d" % (v, gi)]
            ctx["g"] = gi
            G["kn"], G["kw"] = kn, kw
            bk = ("pb", "pw")[gi & 1]
            pa, pz, kz = T[bk][:, 256 + G["t0"]:256 + G["t1"]], T[bk][:, sl], ["pb%d" % gi]
            if par["wc"]:
                mm([(pa, T.idf[:], stw(v, G), True, True, 4 * n)], ["idf"] + kw, ["pw%d" % gi], bk, "wcopy")
                tt(T.rf[:, sl], stn(v, G), pa, A_.mult, kn + ["pw%d" % gi], ["rf%d" % gi], n, 1.0, [bk], "prodF")
            else:
                tt(T.rf[:, sl], stn(v, G), stw(v, G), A_.mult, kn + kw, ["rf%d" % gi], n, 2.0, name="prodF")
            ts(T.rf[:, sl], T.rf[:, sl], 4095, A_.bitwise_and, ["rf%d" % gi], ["rf%d" % gi], n, name="andF")
            cp(lf[:, sl], T.rf[:, sl], ["rf%d" % gi], ["lf%d_%d" % (v & 1, gi)], n, name="u16F")
            bs, ka = sb[:, 768 + G["t0"]:768 + G["t1"]], ["pw%d" % gi]
            if gi in par["wv"]:
                mm([(pz, T.Dm[:], stw(v, G), True, False, 4 * n), (pz, T.idb[:], bs, False, False, n),
                    (pz, T.c192[0:2, :], T.onb[0:2, 0:n], False, False, n)], ["Dm", "idb", "c192", "onb"] + kw + kB, kz, bk, "w0b")
                mm([(pz, T.arow[0:1, :], T.onb[0:1, 0:n], False, True, n)], ["arow", "onb"], kz, bk, "w0bA")
                if gi in par["hv"]:
                    ts(T.hb[:, sl], pz, -0.515625, A_.add, kz, ["hb%d" % gi], n, bank=[bk], name="h")
                else:
                    act(T.hb[:, sl], pz, ACT.Identity, kz, ["hb%d" % gi], n, bias=-0.515625, bank=[bk], name="h")
                tt(pz, pz, T.hb[:, sl], A_.subtract, kz + ["hb%d" % gi], kz, n, 1.0, [bk], "wb")
            else:
                mm([(pa, T.Dm[:], stw(v, G), True, False, 4 * n), (pa, T.idb[:], bs, False, False, n)], ["Dm", "idb"] + kw + kB, ka, bk, "w0b")
                mm([(pa, T.arow[0:1, :], T.onb[0:1, 0:n], False, True, n)], ["arow", "onb"], ka, bk, "w0bA")
                if gi in par["hv"]:
                    ts(T.hb[:, sl], pa, 192.0, A_.add, ka, ["hb%d" % gi], n, bank=[bk], name="h")
                else:
                    act(T.hb[:, sl], pa, ACT.Identity, ka, ["hb%d" % gi], n, bias=192.0, bank=[bk], name="h")
                mm([(pz, T.Dm[:], stw(v, G), True, False, 4 * n), (pz, T.idb[:], bs, False, False, n),
                    (pz, T.arow[0:1, :], T.onb[0:1, 0:n], False, False, n), (pz, T.c192[0:2, :], T.onb[0:2, 0:n], False, False, n),
                    (pz, T.idn[:], T.hb[:, sl], False, True, n)],
                   ["Dm", "idb", "arow", "c192", "onb", "idn", "hb%d" % gi] + kw + kB, kz, bk, "wb")
            tt(T.rb[:, sl], stn(v, G), pz, A_.mult, kn + kz, ["rb%d" % gi], n, 1.0, [bk], "prodB")
            ts(T.rb[:, sl], T.rb[:, sl], 4095, A_.bitwise_and, ["rb%d" % gi], ["rb%d" % gi], n, name="andB")
            cp(T.lb[:, sl], T.rb[:, sl], ["rb%d" % gi], ["lb%d" % gi], n, name="u16B")
            dzo = T.db[:, 2 * G["t0"] + n:2 * G["t1"]]
            if par["dzs"]:
                mm([(pa, T.idm[:], stw(v, G), True, False, 4 * n), (pa, T.idb[:], bs, False, False, n),
                    (pa, T.arow[0:1, :], T.onb[0:1, 0:n], False, False, n), (pa, T.c192[0:2, :], T.onb[0:2, 0:n], False, False, n),
                    (pa, T.idn[:], T.hb[:, sl], False, True, n)],
                   ["idm", "idb", "arow", "c192", "onb", "idn", "hb%d" % gi] + kw + kB, ka, bk, "dzm")
                act(dzo, pa, ACT.Identity, ka, ["dz%d" % gi], n, bank=[bk], name="dz")
            else:
                tt(dzo, pz, stw(v, G), A_.subtract, kz + kw, ["dz%d" % gi], n, 1.0, [bk], "dz")
        mm([(T.pu[:, 0:16], T.ZW[:, 15 - r:143 - r], sb[:, r:256:16], r == 0, r == 15, 64) for r in range(16)],
           ["ZW"] + kS, ["pu_s"], "pu", "usmm")
        act(T.us[:], T.pu[:, 0:16], ACT.Identity, ["pu_s", "CW"], ["us"], 16, bias=CW, scale=-1.0, bank=["pu"], name="us")
        for gi, G in enumerate(grp):
            pk, kk = T["pk%d" % (gi & 1)], "pk%d" % (gi & 1)
            for ci in G["cs"]:
                c = chunks[ci]
                ctx.update({"g": gi, "c": ci})
                n, p, t0, t1 = c["n"], c["pos"], c["t0"], c["t1"]
                e = p + 16 * n
                Fk, Bk = ["F%d" % ci, "Fl%d" % ci, "Fa%d" % ci], ["B%d" % ci, "Bl%d" % ci, "Ba%d" % ci]
                Fp = "Fpad%d" % gi if c["first"] else "Fl%d" % (ci - 1)
                Bp = "Bpad%d" % gi if c["first"] else "Bl%d" % (ci - 1)
                for kind, buf, lst_, lk, wk in (("F", T.F, lf, "lf%d_%d" % (v & 1, gi), Fk), ("B", T.B, T.lb, "lb%d" % gi, Bk)):
                    pieces = [(0, n, wk)]
                    if (kind, ci) in par["cut"]:
                        pieces = [(0, n // 2, wk[2:]), (n // 2, n, wk[:2])]
                    for h, (i0, i1, wk2) in enumerate(pieces):
                        win = T.x[:, 0:4096].indirect(lst_[:, t0 + i0:t0 + i1])
                        o, nm = buf[:, p + 16 * i0:p + 16 * i1], "g%s%d%s" % (kind, ci, "ab"[h])
                        if (kind, ci) in par["gv"] or (kind, ci, h) in par["gv"]:
                            cp(o, win, XK + [lk], wk2, 16 * (i1 - i0), gc_, name=nm)
                        else:
                            act(o, win, ACT.Identity, XK + [lk], wk2, 16 * (i1 - i0), c=gc_, name=nm)
                slF, slB = T.F[:, p - 1:e - 16:16], T.B[:, p - 1:e - 16:16]
                Fb, Bb = [Fp, Fk[0], Fk[2]], [Bp, Bk[0], Bk[2]]
                gcp(T.svF[:, t0:t1], slF, Fb, ["svF%d" % ci], n, "saveF")
                add("V", vc(16 * n, 0.5), Fb[1:] + ["pmask"], ["PX%d" % ci],
                    lambda p=p, e=e, n=n: V.tensor_tensor_scan(T.PX[:, p + 1:e], T.F[:, p:e - 1], T.pmask[:, 0:16 * n - 1], 0.0,
                                                               A_.add, A_.mult), name="scanP%d" % ci)
                gcp(slF, sb[:, 256 + t0:256 + t1], kH, Fb, n, "hi")
                pc, kc = T["pc%d" % (ci & 1)], "pc%d" % (ci & 1)
                mm([(pc[:, 0:n], T.idb[:], sb[:, 512 + t0:512 + t1], True, False, n),
                    (pc[:, 1:n], T.idn[:], T.PX[:, p + 15:e - 16:16], False, False, n)],
                   ["idb", "idn", "PX%d" % ci] + kL, [kc], kc, "corr0")
                lst = [(pc[:, 0:n], T.idb[:], T.B[:, p + j:e:16], False, False, max(n, 64)) for j in range(16)]
                lst.append((pc[:, 1:n], T.idn[:], T.B[:, p + 15:e - 16:16], False, True, max(n, 64)))
                mm(lst, ["idb", "idn"] + Bk, [kc], kc, "corr%d" % ci)
                gcp(T.svB[:, t0:t1], slB, Bb, ["svB%d" % ci], n, "saveB")
                if ci in par["ev"]:
                    ts(slB, pc[:, 0:n], -1.0, A_.mult, [kc], Bb, n, bank=[kc], name="evac")
                else:
                    act(slB, pc[:, 0:n], ACT.Identity, [kc], Bb, n, scale=-1.0, bank=[kc], name="evac")
                add("V", vc(16 * n, 0.5), Fb + Bb, ["Y%d" % ci],
                    lambda p=p, e=e: V.tensor_tensor_scan(T.Y[:, p:e], T.F[:, p - 1:e - 1], T.B[:, p - 1:e - 1], 0.0,
                                                          A_.add, A_.subtract), name="scanY%d" % ci)
                q0, q1 = t0 // 16, t1 // 16
                ko = pk[:, t0 - G["t0"]:t1 - G["t0"]]
                lo_, hi_ = t0 - G["t0"], t1 - G["t0"]
                if ci in par["ab"]:
                    ts(T.Y[:, p:e], T.Y[:, p:e], 255.0, A_.min, ["Y%d" % ci], ["Y%d" % ci], 16 * n, c=0.5, name="zm%d" % ci)
                    act(T.Zp[:, q0:q1], T.Y[:, p:e], ACT.Abs, ["Y%d" % ci], ["Zp%d" % ci], 16 * n, name="za%d" % ci)
                    mm([(ko, T.idb[:], T.kh[:, lo_:hi_], True, False, n), (ko, T.idb[:], T.kl[:, lo_:hi_], False, False, n)],
                       ["idb", "kh", "kl"], [kk], kk, "key0")
                    mm([(ko, T.Zpos[:, 15 - r:143 - r], T.Zp[:, q0:q1, r, :], False, r == 15, max(n, 64)) for r in range(16)],
                       ["Zpos", "Zp%d" % ci], [kk], kk, "keyp")
                    continue
                ts(T.Zp[:, q0:q1], T.Y[:, p:e], 0.0, A_.max, ["Y%d" % ci], ["Zp%d" % ci], 16 * n, 255.0, A_.min, 0.5, name="zp%d" % ci)
                if ci in par["zs"]:
                    act(T.Zn[:, q0:q1], T.Y[:, p:e], ACT.Relu, ["Y%d" % ci], ["Zn%d" % ci], 16 * n, scale=-1.0, name="zn%d" % ci)
                    Zw = T.Zpos
                else:
                    ts(T.Zn[:, q0:q1], T.Y[:, p:e], 0.0, A_.min, ["Y%d" % ci], ["Zn%d" % ci], 16 * n, c=0.5, name="zn%d" % ci)
                    Zw = T.Zneg
                lst = [(ko, T.idb[:], T.kh[:, lo_:hi_], True, False, n), (ko, T.idb[:], T.kl[:, lo_:hi_], False, False, n)]
                mm(lst, ["idb", "kh", "kl"], [kk], kk, "key0")
                mm([(ko, T.Zpos[:, 15 - r:143 - r], T.Zp[:, q0:q1, r, :], False, False, max(n, 64)) for r in range(16)],
                   ["Zpos", "Zp%d" % ci], [kk], kk, "keyp")
                mm([(ko, Zw[:, 15 - r:143 - r], T.Zn[:, q0:q1, r, :], False, r == 15, max(n, 64)) for r in range(16)],
                   ["Zpos", "Zneg", "Zn%d" % ci], [kk], kk, "keyn")
            n, p, t0, t1 = G["n"], G["pos"], G["t0"], G["t1"]
            e = p + 16 * n
            sl, qs, Q, s = slice(t0, t1), slice(G["q0"], G["q1"]), G["q1"] - G["q0"], str(gi)
            Fall = [k % ci for ci in G["cs"] for k in ("Fa%d", "F%d", "Fl%d")]
            Ball = [k % ci for ci in G["cs"] for k in ("Ba%d", "B%d", "Bl%d")]
            gcp(T.F[:, p + 15:e - 16:16], T.svF[:, t0 + 1:t1], ["svF%d" % ci for ci in G["cs"]], Fall[:-1], n - 1, "restF")
            gcp(T.B[:, p + 15:e - 16:16], T.svB[:, t0 + 1:t1], ["svB%d" % ci for ci in G["cs"]], Ball[:-1], n - 1, "restB")
            add("V", vc(n), [kk, "rst"], ["ms" + s],
                lambda sl=sl, n=n, pk=pk: V.tensor_tensor_scan(T.ms[:, sl], T.rst[:, 0:n], pk[:, 0:n], 0.0, A_.add, A_.min),
                [kk], name="minscan")
            mk = T.ms[:, t0 + 15:t1:16]
            tt(T.nok[:, qs], mk, T.thk[:, qs], A_.is_gt, ["ms" + s, "thk"], ["nok" + s], Q, name="nok")
            if gi in par["k1"]:
                tt(T.ki[:, qs], mk, T.nok[:, qs], A_.add, ["ms" + s, "nok" + s], ["ki" + s], Q, name="ki")
            else:
                cp(T.ki[:, qs], mk, ["ms" + s], ["ki" + s], Q, name="ki")
            ts(T.of[:, qs], T.ki[:, qs], 4095, A_.bitwise_and, ["ki" + s], ["of" + s], Q, 1, A_.logical_shift_right, name="of")
            cp(T.l1[:, qs], T.of[:, qs], ["of" + s], ["l1" + s], Q, name="l1")
            if gi in par["k1"]:
                ts(T.cd[:, qs], T.ki[:, qs], 31, A_.bitwise_and, ["ki" + s], ["cd" + s], Q, name="cd")
            else:
                ts(T.k2[:, qs], T.ki[:, qs], 31, A_.bitwise_and, ["ki" + s], ["k2" + s], Q, name="k2")
                tt(T.cd[:, qs], T.k2[:, qs], T.nok[:, qs], A_.add, ["k2" + s, "nok" + s], ["cd" + s], Q, name="cd")
            cp(T.l2[:, qs], T.cd[:, qs], ["cd" + s], ["l2" + s], Q, name="l2")
            if not last:
                mm([(T.pm[0:Q, 128:256], T.nok[:, qs], T.o256[:], gi == 0, gi == NG - 1, 128)], ["nok" + s, "o256"], ["pm8"], "pm", "count")
            PXall = [k % ci for ci in G["cs"] for k in ("PX%d", "PX0%d")]
            tt(T.mp[:, sl], T.PX[:, p:e].indirect(T.l1[:, qs]), sb[:, sl], A_.min, PXall + ["l1" + s] + kS, ["mp" + s], n, gc_, name="mp")
            uo = T.pu[:, 16 + G["q0"]:16 + G["q1"]]
            mm([(uo, T.idb[:], T.nok[:, qs], True, False, 64)], ["idb", "nok" + s], ["pu" + s], "pu", "umm0")
            mm([(uo, T.ZW[:, 15 - r:143 - r], T.mp[:, t0 + r:t1:16], False, r == 15, 64) for r in range(16)],
               ["ZW", "mp" + s], ["pu" + s], "pu", "umm")
            tt(T.ui[:, qs], uo, T.us[:, qs], A_.add, ["pu" + s, "us"], ["ui" + s], Q, bank=["pu"], name="ui")
            ts(T.u9[:, qs], T.ui[:, qs], 1022, A_.bitwise_and, ["ui" + s], ["u9" + s], Q, name="u9")
            ts(T.l3[:, qs], T.u9[:, qs], 1.0, A_.add, ["u9" + s], ["l3" + s], Q, name="l3")
            ts(T.u4[:, qs], T.ui[:, qs], 1, A_.logical_shift_right, ["ui" + s], ["u4" + s], Q, 15, A_.bitwise_and, name="u4")
            tt(T.y4[:, qs], T.u4[:, qs], T.rbase[:, qs], A_.add, ["u4" + s, "rbase"], ["y4" + s], Q, name="y4")
            w0 = 0
            if last:
                w0 = (16 * t0 + ROT) // 16 * 16
            elif 16 * t1 + ROT > 4096:
                ts(T.y4[:, qs], T.y4[:, qs], 4095, A_.bitwise_and, ["y4" + s], ["y4" + s], Q, name="y4and")
            G["w0"] = w0
            ts(T.l4[:, qs], T.y4[:, qs], float(-w0), A_.add, ["y4" + s], ["l4" + s], Q, name="l4")
            act(T.fk[:, sl], T.F[:, p:e].indirect(T.l1[:, qs]), ACT.Identity, Fall + ["l1" + s], ["fk" + s], n, c=gc_, name="fk")
            act(T.fb[:, sl], T.B[:, p:e].indirect(T.l1[:, qs]), ACT.Identity, Ball + ["l1" + s], ["fb" + s], n, c=gc_, name="fb")
            mm([(pk[:, 0:n], T.idb[:], T.fk[:, sl], True, False, n), (pk[:, 0:n], T.idb[:], T.fb[:, sl], False, True, n)],
               ["idb", "fk" + s, "fb" + s], [kk], kk, "fbsum")
            act(T.av[:, sl], pk[:, 0:n], ACT.Identity, [kk], ["av" + s], n, bias=191.75, scale=0.5, bank=[kk], name="av")
            a0, a1, a2 = 2 * t0, 2 * t0 + n, 2 * t1
            tt(eb[:, a1:a2], T.M1[:].indirect(T.l2[:, qs]), T.db[:, a1:a2], A_.mult, ["M1", "l2" + s, "dz" + s], ["ez%d_%d" % (v, gi)], n,
               gc_, name="ez")
            tt(T.db[:, a0:a1], T.cn[:].indirect(T.l3[:, qs]), stn(v, G), A_.subtract, ["cn", "l3" + s] + G["kn"], ["dl" + s], n,
               gc_, name="dl")
            M2 = T.M3 if last else T.M2
            tt(eb[:, a0:a1], M2[:].indirect(T.l2[:, qs]), T.db[:, a0:a1], A_.mult, ["M2", "M3", "l2" + s, "dl" + s],
               ["el%d_%d" % (v, gi)], n, gc_, name="el")
            dst = (rank - STEP * v) % nr if last else (rank + STEP) % nr
            if last:
                act(T.oL[:, sl], stn(v, G), ACT.Identity, G["kn"], ["oL" + s], n, bias=-148.0009765625, scale=1.0 / 64, name="oL")
                last_send = send(dst, [stw(v, G), eb[:, a1:a2]], stw(NV, G), G["kw"] + ["ez%d_%d" % (v, gi)], "st%d_%d" % (NV, gi),
                                 512 * n, "homew%d" % gi, last_send)
                last_send = send(dst, [T.oL[:, sl], eb[:, a0:a1]], stn(NV, G), ["oL" + s, "el%d_%d" % (v, gi)], "home%d" % gi,
                                 512 * n, "homen%d" % gi, last_send)
                continue
            if gi in par["sp"]:
                last_send = send(dst, [stw(v, G), eb[:, a1:a2]], stw(v + 1, G), G["kw"] + ["ez%d_%d" % (v, gi)],
                                 "st%d_%d" % (v + 1, gi), 512 * n, "dynw", last_send)
                last_send = send(dst, [stn(v, G), eb[:, a0:a1]], stn(v + 1, G), G["kn"] + ["el%d_%d" % (v, gi)],
                                 "sn%d_%d" % (v + 1, gi), 512 * n, "dynn", last_send)
                continue
            last_send = send(dst, [T["st%d" % v][:, a0:a2], eb[:, a0:a2]], T["st%d" % (v + 1)][:, a0:a2],
                             G["kn"] + G["kw"] + ["ez%d_%d" % (v, gi), "el%d_%d" % (v, gi)], "st%d_%d" % (v + 1, gi), 1024 * n,
                             "dyn%d_%d" % (v, gi), last_send)
        if not last:
            Q = grp[0]["q1"]
            act(T.c8[0:Q, :], T.pm[0:Q, 128:256], ACT.Identity, ["pm8"], ["c8"], 128, bank=["pm"], name="c8")
            mm([(T.pm[0:1, 0:128], T.m32[0:1, 0:1], T.onb[0:1, 0:128], True, False, 128),
                (T.pm[0:1, 0:128], T.onb[0:Q, 0:1], T.c8[0:Q, :], False, True, 128)], ["m32", "onb", "c8"], ["pm"], "pm", "csum")
            act(T.cq[0:1, :], T.pm[0:1, 0:128], ACT.Identity, ["pm"], ["cq"], 128, bias=-15.5 / 256, bank=["pm"], name="cq")
            tt(T.arow[0:1, :], T.pm[0:1, 0:128], T.cq[0:1, :], A_.subtract, ["pm", "cq"], ["arow"], 128, 1.0, ["pm"], "arow")
        for gi, G in enumerate(grp):
            s, sl, qs = str(gi), slice(G["t0"], G["t1"]), slice(G["q0"], G["q1"])
            if last:
                w1 = G["w0"] + 16 * G["n"] + 16
                wk = ["xs%d" % gi] + (["xs%d" % (gi + 1)] if gi + 1 < NG else ["xw"])
                tt(T.x[:, G["w0"]:w1].indirect(T.l4[:, qs]), T.av[:, sl], T.m192[:, 0:G["n"]], A_.add, ["l4" + s, "av" + s, "m192"],
                   wk + ["xg"], G["n"], sc_, name="scx")
                c0 = ROT if gi == 0 else G["w0"]
                c1 = grp[gi + 1]["w0"] if gi + 1 < NG else 4096 + ROT
                dma("Y", T.yx[:, c0 - ROT:c1 - ROT], T.x[:, c0:c1], ["xs%d" % gi] + ([] if gi + 1 < NG else ["xw"]), [], 256 * (c1 - c0), "yx")
            else:
                tt(T.x[:, 0:4096].indirect(T.l4[:, qs]), T.av[:, sl], T.m192[:, 0:G["n"]], A_.add, ["l4" + s, "av" + s, "m192"], XK,
                   G["n"], sc_, name="scx")
        allg = lambda k: [k + str(i) for i in range(NG)]
        ts(T.u1[:], T.ui[:], 3, A_.bitwise_and, allg("ui"), ["u1"], 16, name="u1")
        tt(T.c3[:], T.u1[:], T.cbase[:], A_.add, ["u1", "cbase"], ["c3"], 16, name="c3")
        cp(T.l5[:], T.c3[:], ["c3"], ["l5"], 16, name="l5")
        for gi, G in enumerate(grp):
            cp(T.cn[:].indirect(T.l5[:, G["q0"]:G["q1"]]), stn(v, G), ["l5"] + G["kn"], ["cn"], G["n"], sc_, name="scc")

    act(T.oC[:], T.cn[:, 1:1024:2], ACT.Identity, ["cn"], ["oC"], 512, bias=-148.0009765625, scale=1.0 / 64, name="oC")
    dma("Y", T.yc[:], T.oC[:], ["oC"], [], 262144, "yc")
    for gi, G in enumerate(grp):
        n, sl, s, k = G["n"], slice(G["t0"], G["t1"]), str(gi), ["st%d_%d" % (NV, gi)]
        bk = ("pw", "pb")[gi & 1]
        pt = T[bk][:, 0:n]
        mm([(pt, T.c45[0:1, :], T.onb[0:1, 0:n], True, False, n), (pt, T.sel0[0:8, :], T.abb[0:8, sl], False, False, n)],
           ["c45", "onb", "sel0", "ab"], [z + str(i) for i in range(NG) for z in ("pb", "pw")][:0] + [bk + "0"], bk, "fin0")
        mm([(pt, T.Dd[:], stw(NV, G), False, True, 4 * n)], ["Dd"] + k, [bk + "0"], bk, "fin1")
        ts(T.ng[:, sl], pt, 0.0, A_.is_lt, [bk + "0"], ["ng" + s], n, 256.0, A_.mult, bank=[bk], name="ng")
        tt(T.oT[:, sl], pt, T.ng[:, sl], A_.add, [bk + "0", "ng" + s], ["oT" + s], n, 1.0, [bk], "oT")
        dma("Y", T.yt[:, sl], T.oT[:, sl], ["oT" + s], [], 512 * n, "yt")
        dma("S", T.yl[:, sl], stn(NV, G), ["home" + s], [], 512 * n, "yl")
    return ops


def depend(ops):
    lastw, readers, bank = {}, {}, {}
    for i, o in enumerate(ops):
        d = {}

        def need(j, hard):
            if j is not None and j != i:
                if ops[j]["eng"] == "P" and o["eng"] == "P":
                    hard = False
                d[j] = d.get(j, False) or hard
        for k in o["rd"]:
            need(lastw.get(k), True)
        for k in o["wr"]:
            need(lastw.get(k), True)
            for j in readers.get(k, []):
                need(j, True)
        for b in o["bank"]:
            j = bank.get(b)
            if j is not None:
                need(j[0], ops[j[0]]["eng"] != o["eng"])
                if j[1] is not None:
                    need(j[1], ops[j[1]]["eng"] != o["eng"])
            other = None if j is None else (j[0] if ops[j[0]]["eng"] != o["eng"] else j[1])
            bank[b] = (i, other)
        need(o["after"], False)
        for k in o["rd"]:
            readers.setdefault(k, []).append(i)
        for k in o["wr"]:
            lastw[k] = i
            readers[k] = []
        o["dep"] = d


def gaps(ops, lat):
    out = []
    for o in ops:
        out.append([(j, ops[j]["dur"] + ((ops[j]["lat"] + lat) if hard else 0.0)) for j, hard in o["dep"].items()])
    return out


def place(n, eng, dur, pred, succ, key, first=None):
    left = [len(p) for p in pred]
    ready = [i for i in range(n) if left[i] == 0]
    beg = [0.0] * n
    busy = {}
    while ready:
        a = min(ready, key=lambda i: key[i])
        ready.remove(a)
        s = first[a] if first else 0.0
        for j, d in pred[a]:
            if beg[j] + d > s:
                s = beg[j] + d
        if eng[a] is not None:
            iv = busy.setdefault(eng[a], [])
            k = len(iv)
            while k > 0 and iv[k - 1][1] > s:
                k -= 1
            while k < len(iv) and iv[k][0] < s + dur[a]:
                s = max(s, iv[k][1])
                k += 1
            iv.insert(k, (s, s + dur[a]))
        beg[a] = s
        for j, _d in succ[a]:
            left[j] -= 1
            if left[j] == 0:
                ready.append(j)
    return beg


LATE = {"scc": 6.0, "us": 3.0, "usmm": 3.0, "dz": 3.0, "dzm": 3.0, "u1": 5.0, "c3": 5.0, "l5": 5.0}


def first_keys(ops):
    key = []
    first = {}
    for o in ops:
        if o["name"][:2] == "gF":
            first.setdefault(o["at"][1], o["at"][2])
    for i, o in enumerate(ops):
        v, gi, ci = o["at"]
        nm = o["name"]
        if nm in ("wcopy", "prodF", "andF", "u16F", "w0b", "w0bA", "h", "wb", "prodB", "andB", "u16B", "dz", "dzm"):
            k = 3.3 * first[gi] - 3.5
        elif nm[:2] == "gF":
            k = 3.3 * ci - 1.7
        elif nm[:2] == "gB":
            k = 3.3 * ci
        elif nm[:4] in ("stat", "arrs", "us", "usmm"):
            k = 0.0
        elif nm == "saveF" or nm == "hi" or nm == "corr0" or nm[:5] == "scanP":
            k = 3.3 * ci + 0.1
        elif nm[:4] in ("corr", "save", "evac") or nm[:5] == "scanY":
            k = 3.3 * ci + 1.55
        elif nm[0] == "z" or nm[:3] == "key":
            k = 3.3 * ci + 3.0
        else:
            k = 3.3 * ci + 4.8
        key.append(20.0 * v + k + LATE.get(nm, 0.0) + 1e-3 * i)
    return key


def span(ops, pred, order):
    beg, free, end = [0.0] * len(ops), {}, 0.0
    for i in order:
        o = ops[i]
        s = free.get(o["eng"], 0.0)
        for j, d in pred[i]:
            if beg[j] + d > s:
                s = beg[j] + d
        beg[i] = s
        if o["eng"] is not None:
            free[o["eng"]] = s + o["dur"]
        end = max(end, s + o["dur"] + o["lat"])
    return end, beg


def improve(variants, lat, rounds, seed):
    ops = variants[0]
    n = len(ops)
    eng, dur = [o["eng"] for o in ops], [o["dur"] for o in ops]
    preds = [gaps(v, l) for v, l in zip(variants, lat)]
    pred = preds[0]
    succ = [[] for _ in range(n)]
    rpred = [[] for _ in range(n)]
    for i in range(n):
        for j, d in pred[i]:
            succ[j].append((i, d))
            rpred[j].append((i, d - dur[j] + dur[i]))
    tail = [o["lat"] for o in ops]
    rng = np.random.default_rng(seed)
    key = first_keys(ops)
    best, cur, bkey, border = 1e9, 1e9, key, None
    tag = np.array([o["name"] for o in ops])
    names = sorted(set(tag.tolist()))
    starts = [i for i in range(1, n) if ops[i - 1]["at"][0] >= 0 and (i < 2 or ops[i - 2]["at"][0] != ops[i - 1]["at"][0])]
    per = starts[2] - starts[1]
    for it in range(rounds):
        passes = 0
        if it:
            k = np.array(bkey)
            mode = int(rng.integers(0, 5))
            if mode == 4:
                a, b = [starts[int(x)] - 1 for x in rng.choice(3, 2, replace=False)]
                k[b:b + per] = k[a:a + per] + float(np.median(k[b:b + per] - k[a:a + per]))
            elif mode == 0:
                k = k + rng.normal(0.0, float(rng.choice([0.1, 0.3, 1.0])), n) * (rng.random(n) < 0.2)
            elif mode == 1:
                for nm in rng.choice(names, int(rng.integers(1, 5))):
                    k = k + rng.normal(0.0, 1.5) * (tag == nm)
            else:
                a = int(rng.integers(0, per))
                w = int(rng.integers(1, 30))
                sh = rng.normal(0.0, 2.0)
                for s in starts:
                    if mode == 2 or rng.random() < 0.4:
                        k[s + a:s + a + w] += sh
            key = [float(x) for x in k]
            passes = int(rng.integers(0, 2))
        for _ in range(passes):
            beg = place(n, eng, dur, pred, succ, key)
            rb = place(n, eng, dur, rpred, pred, [-(beg[i] + dur[i] + tail[i]) for i in range(n)], tail)
            key = [-(rb[i] + dur[i]) for i in range(n)]
        beg = place(n, eng, dur, pred, succ, key)
        order = sorted(range(n), key=lambda i: (beg[i], i))
        val = sum(span(v, p, order)[0] for v, p in zip(variants, preds)) / len(variants)
        if val < cur + 0.6 * (1.0 - it / rounds) * rng.random():
            cur, bkey = val, beg
        if val < best:
            best, border = val, order
    return border, best


def polish(variants, lat, order, rounds, seed):
    ops = variants[0]
    n = len(ops)
    preds = [gaps(v, l) for v, l in zip(variants, lat)]
    eng = [o["eng"] for o in ops]
    durs = [[o["dur"] for o in v] for v in variants]
    tails = [[o["dur"] + o["lat"] for o in v] for v in variants]
    pset = [set(o["dep"]) for o in ops]
    rng = np.random.default_rng(seed)

    def run(order, w):
        pred, dur, tail = preds[w], durs[w], tails[w]
        beg, why, free, lastop = [0.0] * n, [-1] * n, {}, {}
        end, ei = 0.0, -1
        for i in order:
            e = eng[i]
            s, y = free.get(e, 0.0), lastop.get(e, -1)
            for j, d in pred[i]:
                if beg[j] + d >= s:
                    s, y = beg[j] + d, j
            beg[i], why[i] = s, y
            if e is not None:
                free[e], lastop[e] = s + dur[i], i
            if s + tail[i] > end:
                end, ei = s + tail[i], i
        return end, why, ei

    def arcs(res):
        out = []
        for _e, why, i in res:
            while why[i] >= 0:
                if why[i] not in pset[i]:
                    out.append((why[i], i))
                i = why[i]
        return out
    res = [run(order, w) for w in range(len(variants))]
    cur = sum(r[0] for r in res)
    best, border, cand = cur, order, arcs(res)
    for it in range(rounds):
        u, v = cand[int(rng.integers(0, len(cand)))]
        a, b = order.index(u), order.index(v)
        mid = order[a:b + 1]
        if rng.random() < 0.5:
            for _ in range(int(rng.integers(0, 3))):
                k = a - 1
                while k >= 0 and eng[order[k]] != eng[v]:
                    k -= 1
                if k >= 0:
                    a = k
            mid = order[a:b + 1]
            take = {v}
            for i in reversed(mid):
                if i in take:
                    take |= pset[i]
            if mid[0] in take:
                continue
            new = [i for i in mid if i in take] + [i for i in mid if i not in take]
        else:
            for _ in range(int(rng.integers(0, 3))):
                k = b + 1
                while k < n and eng[order[k]] != eng[u]:
                    k += 1
                if k < n:
                    b = k
            mid = order[a:b + 1]
            take = {u}
            for i in mid:
                if pset[i] & take:
                    take.add(i)
            if mid[-1] in take:
                continue
            new = [i for i in mid if i not in take] + [i for i in mid if i in take]
        o2 = order[:a] + new + order[b + 1:]
        res = [run(o2, w) for w in range(len(variants))]
        val = sum(r[0] for r in res)
        if val <= cur + 0.5 * (1.0 - it / rounds) * rng.random():
            order, cur, cand = o2, val, arcs(res)
            if val < best:
                best, border = val, o2
    return border, best / len(variants)


def emit(g, T, ops, order):
    qs = {"V": g.vector, "S": g.scalar, "P": g.tensor, "G": g, "Y": g.sync}
    count = {"V": 0, "S": 0, "P": 0, "G": 0}
    known = {e: {} for e in qs}
    clock = {}
    total = {}
    sent = 0
    for i in order:
        o = ops[i]
        if o["kind"] == "r":
            clock[i] = {o["sem"][0]: o["sem"][1]}
            total[o["sem"][0]] = o["sem"][1]
            continue
        e = o["eng"]
        kn = known[e]
        want = [j for j, hard in o["dep"].items() if hard]
        want.sort(key=lambda j: -ops[j].get("pos", -1))
        for j in want:
            sem, val = ops[j]["sem"]
            if kn.get(sem, 0) < val:
                qs[e].wait_ge(T.sem[sem], val)
                for k2, v2 in clock[j].items():
                    if kn.get(k2, 0) < v2:
                        kn[k2] = v2
        ins = o["fn"]()
        o["pos"] = len(clock)
        if o["kind"] == "s":
            sent += o["ne"]
            clock[i] = dict(kn)
            continue
        if o["kind"] == "c":
            count[e] += 1
            o["sem"] = ("c" + e, count[e])
            ins.then_inc(T.sem["c" + e], 1)
        else:
            ins.then_inc(T.sem[o["sem"][0]], 16)
        clock[i] = dict(kn)
        clock[i][o["sem"][0]] = o["sem"][1]
        total[o["sem"][0]] = o["sem"][1]
    g.wait_ge(T.sem.sent, sent)
    for sem, val in total.items():
        if max(known[e].get(sem, 0) for e in qs) < val:
            g.sync.wait_ge(T.sem[sem], val)


PLAN = {}


def rank_program(g, core, T, topo):
    rank = T.rank_of(core)
    if rank is None:
        return
    variants = make(g, T, topo, core, rank, CHOICE, 1 if "order" in PLAN else len(COSTS))
    if "order" not in PLAN:
        lat = [c["lat"] for c in COSTS]
        PLAN["order"] = polish(variants, lat, improve(variants, lat, ROUNDS, SEED)[0], POLISH, SEED)[0]
    emit(g, T, variants[0], PLAN["order"])


def make(g, T, topo, core, rank, choice, k):
    out = []
    for c in COSTS[:k]:
        par = dict(c)
        par.update(choice)
        ops = build(g, T, topo, core, rank, par)
        depend(ops)
        out.append(ops)
    return out
